import numpy as np, ml_dtypes
CORES = [23,119,17,113]
N = 4
BF = ml_dtypes.bfloat16
S, A, L, M, R, D = 512, 8, 16, 4, 32, 16
def steps(nx, sy):
    g = np.arange(8); s = np.zeros(8, np.int64); place = np.zeros((N * L, 8), np.int64); cnt = np.zeros((N * L, 8), np.int64)
    for i in range(N * L):
        place[i] = sy[i // L, :, i % L].astype(np.int64) * S + s
        v = nx[i // L, g, place[i]].astype(np.int64)
        s = v % S; cnt[i] = v // S
    return place, cnt
def counts(rng, uneven=False):
    k = np.argsort(rng.random((N, 8, S, A)), -1)
    w = rng.integers(0, 2, k.shape) * M if uneven else rng.integers(0, M + 1, k.shape)
    return np.ascontiguousarray(np.where(k <= M, k, w).transpose(0, 1, 3, 2))
def perms(rng):
    return np.argsort(rng.random((N, 8, A, S)), -1)
def bounds(rng):
    e = np.zeros((8, N + 1), np.int64)
    e[:, 1:N] = np.arange(1, N) * R + rng.integers(-D, D + 1, (8, N - 1)); e[:, N] = N * R - rng.integers(0, D + 1, 8)
    e[0, N] = N * R - D; e[7, N] = N * R
    return e
def draw(rng, to, ct, e, burst=False):
    n = (e[:, 1:] - e[:, :-1])[:, :, None]
    k = (np.arange(L * M) - M * rng.integers(0, L, (8, N, 1))) % (L * M) if burst else np.argsort(rng.random((8, N, L * M)), -1)
    c = np.sum((k < n).reshape(8, N, L, M), axis=-1)
    g = np.arange(8); s = np.zeros(8, np.int64); sy = np.zeros((N, 8, L), np.int32)
    for i in range(N * L):
        q = i // L; ok = ct[q][g, :, s] == c[:, q, i % L][:, None]
        a = np.argmax(np.where(ok, rng.random((8, A)), -1.0), axis=1)
        sy[q, :, i % L] = a; s = to[q][g, a, s]
    return {"nx": (ct * S + to).reshape(N, 8, A * S).astype(np.int32), "em": rng.integers(0, 64 ** M, (N, 8, A * S)).astype(np.int32), "sy": sy}
def setup_inputs(rng):
    to = np.where(rng.random((N, 8, A, 1)) < 0.125, rng.integers(0, S, (N, 8, A, S)), perms(rng))
    return draw(rng, to, counts(rng), bounds(rng))
def setup_inputs_edge(rng):
    e = bounds(rng); g = np.arange(8)[:, None]; r = np.arange(1, N)[None, :]
    e[:, 1:N] = r * R + D * np.where(g % 2 == 0, 1 - 2 * ((r + g // 2) % 2), 1 - 2 * (g // 2 % 2)); e[:, N] = N * R - D * (np.arange(8) // 4)
    return draw(rng, perms(rng), counts(rng), e)
def setup_inputs_even(rng):
    e = bounds(rng); e[:] = np.arange(N + 1) * R
    return draw(rng, perms(rng), counts(rng), e)
def setup_inputs_merge(rng):
    kind = (np.argsort(rng.random((N, 8, A)), -1) % 4)[:, :, :, None]; h = (N, 8, A, 1); s = np.arange(S)
    one = np.where(rng.random(h) < 0.5, rng.integers(0, 2, h) * (S - 1), rng.integers(0, S, h))
    to = np.where(kind == 0, one, np.where(kind == 1, s, np.where(kind == 2, (s + 1) % S, rng.integers(0, S, (N, 8, A, S)))))
    return draw(rng, to, counts(rng), bounds(rng))
def setup_inputs_spread(rng):
    to = np.minimum(np.floor(S * rng.random((N, 8, A, S)) ** 6), S - 1).astype(np.int64)
    d = draw(rng, to, counts(rng, True), bounds(rng), True)
    h = (N, 8, A * S); d["em"] = (d["em"] >> np.where(rng.random(h) < 0.5, rng.integers(0, 6 * M, h), 0)).astype(np.int32)
    return d
def check_inputs(d):
    bad = []
    for k, top in (("nx", (M + 1) * S), ("em", 64 ** M), ("sy", A)):
        if d[k].min() < 0 or d[k].max() >= top: bad.append("range of " + k)
    if bad: return bad
    place, cnt = steps(d["nx"], d["sy"])
    off = np.add.accumulate(cnt, 0)[L - 1::L] - R * np.arange(1, N + 1)[:, None]
    if (np.abs(off) > D).any(): bad.append("running totals")
    if (off[-1] > 0).any(): bad.append("whole total")
    return bad
def reference(nx, em, sy):
    place, cnt = steps(nx, sy); g = np.broadcast_to(np.arange(8), (N * L, 8)); r = (np.arange(N * L) // L)[:, None]
    e = em[r, g, place].astype(np.int64); beg = np.add.accumulate(cnt, 0) - cnt
    z = np.full((8, N * R), -1, np.int64)
    for m in range(M):
        on = cnt > m
        z[g[on], beg[on] + m] = ((e >> (6 * m)) & 63)[on]
    return {"y": np.ascontiguousarray(z.reshape(8, N, R).transpose(1, 0, 2)).astype(np.float32)}

@@ -1,0 +1,349 @@
+import numpy as np
+from concourse.bass import DstId, RemoteDMATransfer
+from concourse.mybir import dt, AluOpType, AxisListType, ActivationFunctionType
+
+F, H, I, U = "float32", "bfloat16", "int32", "uint16"
+SCRATCH = {
+    "nxi": ("sbuf", [128, 256], I), "emi": ("sbuf", [128, 256], I), "syr": ("sbuf", [1, 128], I),
+    "syb": ("sbuf", [1, 128], H), "one": ("sbuf", [1, 128], H),
+    "pci": ("sbuf", [128, 2], I), "pf": ("sbuf", [128, 1], F), "igf": ("sbuf", [128, 128], F),
+    "rowf": ("sbuf", [128, 128], F), "io4": ("sbuf", [128, 128], F),
+    "ci4": ("sbuf", [128, 4], I), "cf4": ("sbuf", [128, 4], F), "cols": ("sbuf", [128, 4], F),
+    "bo": ("sbuf", [128, 128], H), "bom": ("sbuf", [128, 128], H), "tri": ("sbuf", [128, 128], H),
+    "tri0": ("sbuf", [128, 128], H), "mask": ("sbuf", [128, 16], F), "gind": ("sbuf", [128, 8], H),
+    "ti": ("sbuf", [128, 256], I), "sel": ("sbuf", [128, 256], H), "tb": ("sbuf", [128, 256], H),
+    "hi": ("sbuf", [128, 256], I), "ci": ("sbuf", [128, 256], I), "ya": ("sbuf", [128, 256], F),
+    "na": ("sbuf", [128, 256], F), "za": ("sbuf", [128, 256], F), "zb": ("sbuf", [128, 256], F),
+    "ec": ("sbuf", [128, 256], F), "self": ("sbuf", [128, 256], F), "selfx": ("sbuf", [128, 256], F),
+    "sel1": ("sbuf", [128, 256], H), "tb1": ("sbuf", [128, 256], H),
+    "selx": ("sbuf", [128, 256], H), "tbx": ("sbuf", [128, 256], H), "ecx": ("sbuf", [128, 256], F),
+    "w": ("sbuf", [128, 512], F), "w1": ("sbuf", [128, 512], F), "wx": ("sbuf", [128, 512], F),
+    "e": ("sbuf", [128, 512], F), "ex": ("sbuf", [128, 512], F),
+    "s1": ("sbuf", [128, 2], U), "zero": ("sbuf", [128, 2], U), "tt": ("sbuf", [128, 960], U),
+    "eea": ("sbuf", [128, 272], F), "eeb": ("sbuf", [128, 272], F),
+    "rc0": ("sbuf", [128, 1], F), "rc1": ("sbuf", [128, 1], F), "rc2": ("sbuf", [128, 1], F),
+    "oc": ("sbuf", [128, 1], F), "oc3": ("sbuf", [128, 1], F),
+    "ysb": ("sbuf", [8, 32], F),
+    "px": ("psum", [128, 512], F), "pwa": ("psum", [128, 512], F), "pwb": ("psum", [128, 512], F),
+    "psw": ("psum", [128, 512], F), "pew": ("psum", [128, 512], F), "pb": ("psum", [128, 512], F),
+    "pc": ("psum", [128, 512], F), "py": ("psum", [128, 512], F),
+}
+for _q in range(4):
+    SCRATCH["qi%d" % _q] = ("sbuf", [128, 2], I)
+    SCRATCH["cb%d" % _q] = ("sbuf", [128, 1], H)
+    SCRATCH["di%d" % _q] = ("sbuf", [128, 4], I)
+    SCRATCH["dp%d" % _q] = ("sbuf", [128, 4], F)
+    SCRATCH["g4%d" % _q] = ("sbuf", [128, 4], F)
+    SCRATCH["ep%d" % _q] = ("sbuf", [128, 4], F)
+    SCRATCH["oh%d" % _q] = ("sbuf", [128, 128], H)
+SEMAPHORES = ["v", "s", "t", "p", "lnx", "lsy", "lem", "st", "loc",
+              "as1", "asel1", "atb1", "aselx", "atbx", "aecx", "arc0", "arc1", "arc2"]
+OP = AluOpType
+AF = ActivationFunctionType
+
+
+def rank_program(g, core, T, topo):
+    r = T.rank_of(core)
+    if r is None:
+        return
+    Q = {"v": g.vector, "s": g.scalar, "t": g.tensor, "p": g, "y": g.sync}
+    cnt = {}
+    seen = {}
+
+    def waits(qn, deps):
+        need = {}
+        for d in deps:
+            if d is not None:
+                need[d[0]] = max(need.get(d[0], 0), d[1])
+        for sn in need:
+            if seen.get((qn, sn), 0) < need[sn]:
+                Q[qn].wait_ge(T.sem[sn], need[sn])
+                seen[(qn, sn)] = need[sn]
+
+    def do(qn, deps, fn):
+        waits(qn, deps)
+        fn().then_inc(T.sem[qn], 1)
+        cnt[qn] = cnt.get(qn, 0) + 1
+        return (qn, cnt[qn])
+
+    def dma(qn, deps, sn, out, in_):
+        waits(qn, deps)
+        Q[qn].dma_start(out, in_).then_inc(T.sem[sn], 16)
+        cnt[sn] = cnt.get(sn, 0) + 16
+        return (sn, cnt[sn])
+
+    def fan(dsts):
+        m = topo.mask(core, T.cores[dsts[0]])
+        for d in dsts[1:]:
+            m &= topo.mask(core, T.cores[d])
+        return m
+
+    def send(deps, dsts, name_out, src, sn):
+        waits("p", deps)
+        m = fan(dsts)
+        ids = []
+        for d in dsts:
+            rid, pid, _ = topo.addr(T.cores[d])
+            ids.append(DstId(rid=rid, pnc=pid))
+        g.remote_dma_fused([RemoteDMATransfer(dst_ids=ids, dma_engine_mask=m, remote_sem=T.sem[sn], srcs=[src],
+                                              dsts=[T[name_out][:] for _ in dsts], alu_op=0)],
+                           local_sem=T.sem.loc)
+        cnt["loc"] = cnt.get("loc", 0) + bin(m).count("1")
+
+    def arrive(src, group, sn):
+        m = topo.mask(T.cores[src], T.cores[group[0]])
+        for d in group[1:]:
+            m &= topo.mask(T.cores[src], T.cores[d])
+        cnt[sn] = bin(m).count("1")
+        return (sn, cnt[sn])
+
+    vec = g.vector
+    l_nx = dma("y", [], "lnx", T.nxi[:], T.nx[:])
+    l_sy = dma("s", [], "lsy", T.syr[:], T.sy[:])
+    l_em = dma("y", [], "lem", T.emi[:], T.em[:])
+
+    c_p = do("p", [], lambda: g.iota(T.pci[:], [[0, 2]], 0, 1))
+    c_ig = do("p", [], lambda: g.iota(T.igf[:], [[1, 8], [0, 16]], 0, 0, allow_small_or_imprecise_dtypes=True))
+    c_pf = do("p", [], lambda: g.iota(T.pf[:], [[0, 1]], 0, 1, allow_small_or_imprecise_dtypes=True))
+    c_row = do("p", [], lambda: g.iota(T.rowf[:], [[1, 128]], 0, 0, allow_small_or_imprecise_dtypes=True))
+    c_io = do("p", [], lambda: g.iota(T.io4[:], [[-1, 4], [1, 32]], 32 * r, 0, allow_small_or_imprecise_dtypes=True))
+    c_one = do("v", [], lambda: vec.memset(T.one[:], 1.0))
+    if r == 0:
+        c_zero = do("v", [], lambda: vec.memset(T.zero[:], 0))
+    do("v", [c_p], lambda: vec.tensor_scalar(T.ci4[:, 0:1], T.pci[:, 0:1], 4, None, OP.arith_shift_right))
+    do("v", [], lambda: vec.tensor_scalar(T.ci4[:, 1:2], T.pci[:, 0:1], 15, None, OP.bitwise_and))
+    do("v", [], lambda: vec.tensor_scalar(T.ci4[:, 2:3], T.pci[:, 0:1], 1, 7, OP.arith_shift_right, OP.bitwise_and))
+    x = do("v", [], lambda: vec.tensor_scalar(T.ci4[:, 3:4], T.pci[:, 0:1], 1, None, OP.bitwise_and))
+    c_cf = do("v", [x], lambda: vec.tensor_copy(T.cf4[:], T.ci4[:]))
+    c_bo = do("v", [c_cf, c_ig], lambda: vec.tensor_scalar(T.bo[:], T.igf[:], T.cf4[:, 0:1], None, OP.is_equal))
+    c_bom = do("v", [c_bo], lambda: vec.tensor_scalar(T.bom[:], T.bo[:], -4.0, None, OP.mult))
+    x = do("v", [], lambda: vec.tensor_scalar(T.cols[:, 2:3], T.cf4[:, 3:4], 100.0, T.cf4[:, 2:3], OP.mult, OP.add))
+    c_k0 = do("v", [], lambda: vec.tensor_scalar(T.cols[:, 0:1], T.cf4[:, 3:4], -100.0, T.cf4[:, 2:3], OP.mult, OP.add))
+    c_k1 = do("v", [x], lambda: vec.tensor_scalar(T.cols[:, 1:2], T.cols[:, 2:3], -100.0, None, OP.add))
+    c_mask = do("v", [c_row], lambda: vec.tensor_scalar(T.mask[:], T.rowf[:, 0:16], T.cf4[:, 1:2], None, OP.is_equal))
+    do("t", [c_bom, c_one], lambda: g.tensor.matmul(T.px[:, 0:128], T.bo[:], T.bom[:], True, False))
+    m_sy = do("v", [l_sy], lambda: vec.tensor_scalar(T.syb[:], T.syr[:], 64.0, None, OP.add))
+    m_x = do("t", [m_sy], lambda: g.tensor.matmul(T.px[:, 0:128], T.one[:], T.syb[:], False, True))
+    m_ti = do("v", [l_nx], lambda: vec.tensor_scalar(T.ti[:], T.nxi[:], 511, None, OP.bitwise_and))
+    m_s0 = do("v", [m_x, c_k0], lambda: vec.tensor_scalar(T.sel[:, 0:128], T.px[:, 0:128], T.cols[:, 0:1], None, OP.is_equal))
+    m_s1 = do("v", [c_k1], lambda: vec.tensor_scalar(T.sel[:, 128:256], T.px[:, 0:128], T.cols[:, 1:2], None, OP.is_equal))
+    m_tb = do("v", [m_ti], lambda: vec.tensor_scalar(T.tb[:], T.ti[:], -256.0, None, OP.add))
+
+    def window_ab(sel, tb, w, deps, bank_free):
+        a = do("t", deps + bank_free, lambda: g.tensor.matmul(T.pwa[:, 0:256], sel[:, 0:128], tb[:], True, True))
+        b = do("t", [], lambda: g.tensor.matmul(T.pwb[:, 0:256], sel[:, 128:256], tb[:], True, True))
+        va = do("v", [a], lambda: vec.tensor_scalar(w[:, 0:256], T.pwa[:, 0:256], 256.0, None, OP.add))
+        sb = do("s", [b], lambda: g.scalar.activation(w[:, 256:512], T.pwb[:, 0:256], AF.Identity, bias=256.0))
+        return [va, sb]
+
+    def window_s(sel, tb, w, deps):
+        do("t", deps, lambda: g.tensor.matmul(T.psw[:, 0:256], sel[:, 0:128], tb[:], True, True))
+        b = do("t", [], lambda: g.tensor.matmul(T.psw[:, 256:512], sel[:, 128:256], tb[:], True, True))
+        return [do("s", [b], lambda: g.scalar.activation(w[:], T.psw[:], AF.Identity, bias=256.0))]
+
+    def code_table():
+        do("v", [l_em], lambda: vec.tensor_scalar(T.hi[:], T.emi[:], 18, None, OP.arith_shift_right))
+        a = do("v", [], lambda: vec.tensor_scalar(T.ci[:], T.nxi[:], 9, None, OP.arith_shift_right))
+        b = do("v", [], lambda: vec.tensor_scalar(T.ya[:], T.nxi[:], 2048.0, 64.0, OP.is_lt, OP.mult))
+        n = do("v", [b], lambda: vec.tensor_tensor(T.na[:], T.hi[:], T.ya[:], OP.min))
+        z = do("v", [n], lambda: vec.tensor_tensor(T.za[:], T.ci[:], T.na[:], OP.subtract))
+        z = do("v", [z], lambda: vec.tensor_scalar(T.zb[:], T.za[:], -4.0, 262144.0, OP.add, OP.mult))
+        return do("v", [z], lambda: vec.tensor_tensor(T.ec[:], T.zb[:], T.emi[:], OP.add))
+
+    def code_mm(sf, ec, deps):
+        do("t", deps, lambda: g.tensor.matmul(T.pew[:, 0:256], sf[:, 0:128], ec[:], True, True))
+        return do("t", [], lambda: g.tensor.matmul(T.pew[:, 256:512], sf[:, 128:256], ec[:], True, True))
+
+    def step(win, deps, tile, x0, j, reg):
+        k = (j - 1) % 16
+        nxt = reg + 16 + 18 * j
+        b = nxt - k
+        d = do("v", deps, lambda: vec.tensor_copy(T.tt[:, b:b + 16], win[:, 0:512].indirect(tile[:, x0:x0 + 1])))
+        return d, nxt
+
+    def run(win, deps, tile, x0, reg, n, hook=None):
+        reads = []
+        d = None
+        for j in range(n):
+            reads.append((tile, x0, d if j else deps))
+            dd = deps if j == 0 else [d]
+            d, nx = step(win, dd, tile, x0, j, reg)
+            tile, x0 = T.tt, nx
+            if hook is not None and j == hook[0]:
+                hook[1]()
+        reads.append((tile, x0, d))
+        return reads
+
+    def follow(reads, ewin, edep, ee):
+        last = None
+        for j in range(16):
+            tile, x0, d = reads[j]
+            dd = d if isinstance(d, list) else [d]
+            b = 0 if j == 0 else 16 * j + 16
+            last = do("s", dd + [edep, c_mask], lambda: g.scalar.activation(
+                ee[:, b:b + 16], ewin[:, 0:512].indirect(tile[:, x0:x0 + 1]), AF.Copy, scale=T.mask[:, j:j + 1]))
+        return last
+
+    def total(ee, last, out):
+        return do("v", [last], lambda: vec.tensor_reduce(out[:], ee[:, 15:271:17], AxisListType.X, OP.add))
+
+    cdep = {}
+    epdep = {}
+    ydep = [None, 0]
+
+    def counts(q, code, dep):
+        qi, cb = T["qi%d" % q], T["cb%d" % q]
+        a = do("v", [dep], lambda: vec.tensor_copy(qi[:, 0:1], code[:]))
+        b = do("v", [a], lambda: vec.tensor_scalar(qi[:, 1:2], qi[:, 0:1], 18, None, OP.arith_shift_right))
+        cdep[q] = do("v", [b], lambda: vec.tensor_scalar(cb[:], qi[:, 1:2], 0.0, 4.0, OP.min, OP.add))
+
+    def digits(q):
+        qi, cb, di = T["qi%d" % q], T["cb%d" % q], T["di%d" % q]
+        dp, g4, ep = T["dp%d" % q], T["g4%d" % q], T["ep%d" % q]
+        do("v", [], lambda: vec.tensor_scalar(di[:, 0:1], qi[:, 0:1], 63, None, OP.bitwise_and))
+        do("v", [], lambda: vec.tensor_scalar(di[:, 1:2], qi[:, 0:1], 6, 63, OP.arith_shift_right, OP.bitwise_and))
+        do("v", [], lambda: vec.tensor_scalar(di[:, 2:3], qi[:, 0:1], 12, 63, OP.arith_shift_right, OP.bitwise_and))
+        d = do("v", [], lambda: vec.tensor_scalar(di[:, 3:4], qi[:, 1:2], 63, None, OP.bitwise_and))
+        do("v", [cdep[q]], lambda: vec.tensor_scalar(g4[:], T.rowf[:, 0:4], cb[:], None, OP.is_lt))
+        x = do("v", [d], lambda: vec.tensor_scalar(dp[:], di[:], 1.0, None, OP.add))
+        epdep[q] = do("v", [x], lambda: vec.tensor_tensor(ep[:], dp[:], g4[:], OP.mult))
+
+    banks = {}
+
+    def base(q, bank, free):
+        banks[q] = bank
+        for n, b in enumerate(range(q)):
+            do("t", [cdep[b], c_bo] + free, lambda: g.tensor.matmul(bank[:, 0:1], T.bo[:], T["cb%d" % b][:], n == 0, False))
+
+    def place(q, final):
+        bank = banks[q]
+        bd = do("t", [cdep[q], c_tri], lambda: g.tensor.matmul(bank[:, 0:1], T.tri[:], T["cb%d" % q][:], q == 0, True))
+        for m in range(4):
+            oh, ep = T["oh%d" % q], T["ep%d" % q]
+            o = do("v", [bd, epdep[q], c_io], lambda: vec.tensor_scalar(
+                oh[:, 32 * m:32 * m + 32], T.io4[:, 32 * m:32 * m + 32], bank[:, 0:1], ep[:, m:m + 1], OP.is_equal, OP.mult))
+            ydep[0] = do("t", [o, c_gi], lambda: g.tensor.matmul(
+                T.py[0:8, 0:32], T.gind[:], oh[:, 32 * m:32 * m + 32], ydep[1] == 0, final and m == 3))
+            ydep[1] += 1
+
+    def late_constants():
+        a = do("v", [c_row, c_pf], lambda: vec.tensor_scalar(T.tri0[:], T.rowf[:], T.pf[:], None, OP.is_gt))
+        gi = do("v", [], lambda: vec.tensor_scalar(T.gind[:], T.rowf[:, 0:8], T.cf4[:, 0:1], None, OP.is_equal))
+        tr = do("v", [a], lambda: vec.tensor_tensor(T.tri[:], T.tri0[:], T.bo[:], OP.mult))
+        return tr, gi
+
+    S1A, S1B = [2, 3], [1]
+    G1, C0, C1, C2 = [2, 3], [2, 3, 1], [2, 3, 0], [3, 1]
+
+    wdep = window_ab(T.sel, T.tb, T.w, [m_s1, m_tb], [])
+    sfd = do("s", [m_s1], lambda: g.scalar.activation(T.self[:], T.sel[:], AF.Copy))
+
+    if r == 0:
+        rd = run(T.w, wdep + [c_zero], T.zero, 0, 0, 16)
+        xs = rd[16][1]
+        send([rd[16][2]], S1A, "s1", T.tt[:, xs:xs + 2], "as1")
+        send([], S1B, "s1", T.tt[:, xs:xs + 2], "as1")
+        ecd = code_table()
+        c_tri, c_gi = late_constants()
+        em = code_mm(T.self, T.ec, [sfd, ecd])
+        ed = do("s", [em], lambda: g.scalar.activation(T.e[:], T.pew[:], AF.Copy))
+        last = follow(rd, T.e, ed, T.eea)
+        oc = total(T.eea, last, T.oc)
+        send([oc], C0, "rc0", T.oc[:], "arc0")
+        counts(0, T.oc, oc)
+        digits(0)
+        base(0, T.pb, [])
+        place(0, False)
+        counts(1, T.rc1, arrive(1, C1, "arc1"))
+        base(1, T.pc, [])
+        digits(1)
+        place(1, True)
+    elif r == 1:
+        send([m_s1], G1, "sel1", T.sel[:], "asel1")
+        send([m_tb], G1, "tb1", T.tb[:], "atb1")
+        ecd = code_table()
+        c_tri, c_gi = late_constants()
+        em = code_mm(T.self, T.ec, [sfd, ecd])
+        ed = do("s", [em], lambda: g.scalar.activation(T.e[:], T.pew[:], AF.Copy))
+        rd = run(T.w, wdep + [arrive(0, S1B, "as1")], T.s1, 0, 0, 15)
+        last = follow(rd, T.e, ed, T.eea)
+        oc = total(T.eea, last, T.oc)
+        send([oc], C1, "rc1", T.oc[:], "arc1")
+        counts(1, T.oc, oc)
+        digits(1)
+        counts(0, T.rc0, arrive(0, C0, "arc0"))
+        base(0, T.pb, [])
+        digits(0)
+        place(0, False)
+        base(1, T.pc, [])
+        place(1, False)
+        base(2, T.px, [m_s1])
+        counts(2, T.rc2, arrive(2, C2, "arc2"))
+        digits(2)
+        place(2, True)
+    else:
+        o = 5 - r
+        send([m_s1], [o], "selx", T.sel[:], "aselx")
+        send([m_tb], [o], "tbx", T.tb[:], "atbx")
+        ecd = code_table()
+        if r == 3:
+            send([ecd], [2], "ecx", T.ec[:], "aecx")
+        c_tri, c_gi = late_constants()
+        a_sx, a_tx = arrive(o, [r], "aselx"), arrive(o, [r], "atbx")
+        a_s1, a_t1 = arrive(1, G1, "asel1"), arrive(1, G1, "atb1")
+        w1dep = window_ab(T.sel1, T.tb1, T.w1, [a_s1, a_t1], wdep)
+        wxdep = window_s(T.selx, T.tbx, T.wx, [a_sx, a_tx])
+        em = code_mm(T.self, T.ec, [sfd, ecd])
+        ed = do("s", [em], lambda: g.scalar.activation(T.e[:], T.pew[:], AF.Copy))
+        rd1 = run(T.w1, w1dep + [arrive(0, S1A, "as1")], T.s1, 0, 0, 16)
+        t2 = rd1[16]
+        wins = {r: (T.w, wdep), o: (T.wx, wxdep)}
+        rd2 = run(wins[2][0], wins[2][1] + [t2[2]], t2[0], t2[1], 320, 16)
+        t3 = rd2[16]
+        if r == 2:
+            last2 = follow(rd2, T.e, ed, T.eea)
+            box = []
+
+            def mid():
+                oc = total(T.eea, last2, T.oc)
+                send([oc], C2, "rc2", T.oc[:], "arc2")
+                box.append(oc)
+            rd3 = run(wins[3][0], wins[3][1] + [t3[2]], t3[0], t3[1], 640, 15, hook=(2, mid))
+            sfx = do("s", [], lambda: g.scalar.activation(T.selfx[:], T.selx[:], AF.Copy))
+            em = code_mm(T.selfx, T.ecx, [sfx, arrive(3, [2], "aecx"), ed])
+            exd = do("s", [em], lambda: g.scalar.activation(T.ex[:], T.pew[:], AF.Copy))
+            last3 = follow(rd3, T.ex, exd, T.eeb)
+            counts(2, T.oc, box[0])
+            digits(2)
+            counts(0, T.rc0, arrive(0, C0, "arc0"))
+            counts(1, T.rc1, arrive(1, C1, "arc1"))
+            base(1, T.pb, [])
+            digits(1)
+            place(1, False)
+            base(2, T.pc, [])
+            place(2, False)
+            base(3, T.px, [m_s1])
+            oc3 = total(T.eeb, last3, T.oc3)
+            counts(3, T.oc3, oc3)
+            digits(3)
+            place(3, True)
+        else:
+            rd3 = run(wins[3][0], wins[3][1] + [t3[2]], t3[0], t3[1], 640, 15)
+            last3 = follow(rd3, T.e, ed, T.eea)
+            oc3 = total(T.eea, last3, T.oc3)
+            counts(3, T.oc3, oc3)
+            digits(3)
+            counts(0, T.rc0, arrive(0, C0, "arc0"))
+            counts(1, T.rc1, arrive(1, C1, "arc1"))
+            counts(2, T.rc2, arrive(2, C2, "arc2"))
+            base(2, T.pb, [])
+            base(3, T.pc, [])
+            digits(2)
+            place(2, False)
+            place(3, True)
+    yd = do("v", [ydep[0]], lambda: vec.tensor_scalar(T.ysb[:], T.py[0:8, 0:32], -1.0, None, OP.add))
+    dma("y", [yd], "st", T.y[:], T.ysb[:])
+    for sn in list(cnt):
+        if sn != "st":
+            waits("p", [(sn, cnt[sn])])
+    waits("p", [("st", 16)])

@@ -5,39 +5,40 @@ from concourse.mybir import dt, AluOpType, AxisListType, ActivationFunctionType
 F, H, I, U = "float32", "bfloat16", "int32", "uint16"
 SCRATCH = {
     "nxi": ("sbuf", [128, 256], I), "emi": ("sbuf", [128, 256], I), "syr": ("sbuf", [1, 128], I),
-    "syb": ("sbuf", [1, 128], H), "one": ("sbuf", [1, 128], H),
+    "syb": ("sbuf", [1, 128], H), "one": ("sbuf", [1, 128], H), "syc": ("sbuf", [128, 1], I),
     "pci": ("sbuf", [128, 2], I), "pf": ("sbuf", [128, 1], F), "igf": ("sbuf", [128, 128], F),
     "rowf": ("sbuf", [128, 128], F), "io4": ("sbuf", [128, 128], F),
-    "ci4": ("sbuf", [128, 4], I), "cf4": ("sbuf", [128, 4], F), "cols": ("sbuf", [128, 4], F),
+    "ci5": ("sbuf", [128, 5], I), "cf5": ("sbuf", [128, 5], F), "cols": ("sbuf", [128, 12], F),
     "bo": ("sbuf", [128, 128], H), "bom": ("sbuf", [128, 128], H), "tri": ("sbuf", [128, 128], H),
-    "tri0": ("sbuf", [128, 128], H), "mask": ("sbuf", [128, 16], F), "gind": ("sbuf", [128, 8], H),
+    "tri0": ("sbuf", [128, 128], H), "mask": ("sbuf", [128, 16], F), "gind": ("sbuf", [128, 8], H), "thr": ("sbuf", [128, 4], F),
+    "idn": ("sbuf", [128, 128], H), "idm": ("sbuf", [128, 1024], H),
     "ti": ("sbuf", [128, 256], I), "sel": ("sbuf", [128, 256], H), "tb": ("sbuf", [128, 256], H),
     "hi": ("sbuf", [128, 256], I), "ci": ("sbuf", [128, 256], I), "ya": ("sbuf", [128, 256], F),
     "na": ("sbuf", [128, 256], F), "za": ("sbuf", [128, 256], F), "zb": ("sbuf", [128, 256], F),
     "ec": ("sbuf", [128, 256], F), "self": ("sbuf", [128, 256], F), "selfx": ("sbuf", [128, 256], F),
-    "sel1": ("sbuf", [128, 256], H), "tb1": ("sbuf", [128, 256], H),
+    "tp": ("sbuf", [128, 256], I), "tpi": ("sbuf", [128, 256], I), "tq": ("sbuf", [128, 288], F), "tab": ("sbuf", [128, 544], F),
+    "d16": ("sbuf", [128, 16], H), "ot": ("sbuf", [128, 16], U), "lt": ("sbuf", [128, 256], U),
     "selx": ("sbuf", [128, 256], H), "tbx": ("sbuf", [128, 256], H), "ecx": ("sbuf", [128, 256], F),
-    "w": ("sbuf", [128, 512], F), "w1": ("sbuf", [128, 512], F), "wx": ("sbuf", [128, 512], F),
+    "w": ("sbuf", [128, 512], H), "w1": ("sbuf", [128, 512], H), "wx": ("sbuf", [128, 512], H),
     "e": ("sbuf", [128, 512], F), "ex": ("sbuf", [128, 512], F),
-    "s1": ("sbuf", [128, 2], U), "zero": ("sbuf", [128, 2], U), "tt": ("sbuf", [128, 960], U),
+    "cp": ("sbuf", [128, 4096], H), "cpm": ("sbuf", [128, 512], H), "cpx": ("sbuf", [128, 512], H),
+    "s1": ("sbuf", [128, 2], U), "zero": ("sbuf", [128, 2], U), "tt": ("sbuf", [128, 1080], U),
     "eea": ("sbuf", [128, 272], F), "eeb": ("sbuf", [128, 272], F),
-    "rc0": ("sbuf", [128, 1], F), "rc1": ("sbuf", [128, 1], F), "rc2": ("sbuf", [128, 1], F),
-    "oc": ("sbuf", [128, 1], F), "oc3": ("sbuf", [128, 1], F),
-    "ysb": ("sbuf", [8, 32], F),
+    "rc0": ("sbuf", [128, 1], F), "rc1": ("sbuf", [128, 1], F),
+    "oca": ("sbuf", [128, 1], F), "ocb": ("sbuf", [128, 1], F), "ysb": ("sbuf", [8, 32], F),
     "px": ("psum", [128, 512], F), "pwa": ("psum", [128, 512], F), "pwb": ("psum", [128, 512], F),
     "psw": ("psum", [128, 512], F), "pew": ("psum", [128, 512], F), "pb": ("psum", [128, 512], F),
     "pc": ("psum", [128, 512], F), "py": ("psum", [128, 512], F),
 }
 for _q in range(4):
-    SCRATCH["qi%d" % _q] = ("sbuf", [128, 2], I)
-    SCRATCH["cb%d" % _q] = ("sbuf", [128, 1], H)
+    SCRATCH["qi%d" % _q] = ("sbuf", [128, 1], I)
     SCRATCH["di%d" % _q] = ("sbuf", [128, 4], I)
     SCRATCH["dp%d" % _q] = ("sbuf", [128, 4], F)
-    SCRATCH["g4%d" % _q] = ("sbuf", [128, 4], F)
+    SCRATCH["g4%d" % _q] = ("sbuf", [128, 4], H)
     SCRATCH["ep%d" % _q] = ("sbuf", [128, 4], F)
     SCRATCH["oh%d" % _q] = ("sbuf", [128, 128], H)
-SEMAPHORES = ["v", "s", "t", "p", "lnx", "lsy", "lem", "st", "loc",
-              "as1", "asel1", "atb1", "aselx", "atbx", "aecx", "arc0", "arc1", "arc2"]
+SEMAPHORES = ["v", "s", "t", "p", "lnx", "lsy", "lsc", "ltp", "lem", "st", "loc",
+              "as1", "aw1", "aselx", "atbx", "aecx", "acpx", "arc0", "arc1"]
 OP = AluOpType
 AF = ActivationFunctionType
 
@@ -49,6 +50,7 @@ def rank_program(g, core, T, topo):
     Q = {"v": g.vector, "s": g.scalar, "t": g.tensor, "p": g, "y": g.sync}
     cnt = {}
     seen = {}
+    vec, act, mm = g.vector, g.scalar.activation, g.tensor.matmul
 
     def waits(qn, deps):
         need = {}
@@ -66,21 +68,25 @@ def rank_program(g, core, T, topo):
         cnt[qn] = cnt.get(qn, 0) + 1
         return (qn, cnt[qn])
 
+    def ts(deps, *a):
+        return do("v", deps, lambda: vec.tensor_scalar(*a))
+
     def dma(qn, deps, sn, out, in_):
         waits(qn, deps)
         Q[qn].dma_start(out, in_).then_inc(T.sem[sn], 16)
         cnt[sn] = cnt.get(sn, 0) + 16
         return (sn, cnt[sn])
 
-    def fan(dsts):
-        m = topo.mask(core, T.cores[dsts[0]])
-        for d in dsts[1:]:
-            m &= topo.mask(core, T.cores[d])
+    def fan(src):
+        m = -1
+        for c in T.cores:
+            if c != T.cores[src]:
+                m &= topo.mask(T.cores[src], c)
         return m
 
     def send(deps, dsts, name_out, src, sn):
         waits("p", deps)
-        m = fan(dsts)
+        m = fan(r)
         ids = []
         for d in dsts:
             rid, pid, _ = topo.addr(T.cores[d])
@@ -90,258 +96,353 @@ def rank_program(g, core, T, topo):
                            local_sem=T.sem.loc)
         cnt["loc"] = cnt.get("loc", 0) + bin(m).count("1")
 
-    def arrive(src, group, sn):
-        m = topo.mask(T.cores[src], T.cores[group[0]])
-        for d in group[1:]:
-            m &= topo.mask(T.cores[src], T.cores[d])
-        cnt[sn] = bin(m).count("1")
+    def arrive(src, sn):
+        cnt[sn] = bin(fan(src)).count("1")
         return (sn, cnt[sn])
 
-    vec = g.vector
     l_nx = dma("y", [], "lnx", T.nxi[:], T.nx[:])
     l_sy = dma("s", [], "lsy", T.syr[:], T.sy[:])
+    if r > 0:
+        l_sc = dma("s", [], "lsc", T.syc[:], T.sy[:])
+        for a in range(8):
+            l_tp = dma("y" if a % 2 else "s", [], "ltp", T.tp[:, 32 * a:32 * a + 32], T.nx[:, 512 * a:512 * a + 512])
     l_em = dma("y", [], "lem", T.emi[:], T.em[:])
 
+    lo = {"allow_small_or_imprecise_dtypes": True}
     c_p = do("p", [], lambda: g.iota(T.pci[:], [[0, 2]], 0, 1))
-    c_ig = do("p", [], lambda: g.iota(T.igf[:], [[1, 8], [0, 16]], 0, 0, allow_small_or_imprecise_dtypes=True))
-    c_pf = do("p", [], lambda: g.iota(T.pf[:], [[0, 1]], 0, 1, allow_small_or_imprecise_dtypes=True))
-    c_row = do("p", [], lambda: g.iota(T.rowf[:], [[1, 128]], 0, 0, allow_small_or_imprecise_dtypes=True))
-    c_io = do("p", [], lambda: g.iota(T.io4[:], [[-1, 4], [1, 32]], 32 * r, 0, allow_small_or_imprecise_dtypes=True))
+    c_ig = do("p", [], lambda: g.iota(T.igf[:], [[1, 8], [0, 16]], 0, 0, **lo))
+    c_pf = do("p", [], lambda: g.iota(T.pf[:], [[0, 1]], 0, 1, **lo))
+    c_row = do("p", [], lambda: g.iota(T.rowf[:], [[1, 128]], 0, 0, **lo))
+    c_io = do("p", [], lambda: g.iota(T.io4[:], [[-1, 4], [1, 32]], 32 * r, 0, **lo))
     c_one = do("v", [], lambda: vec.memset(T.one[:], 1.0))
-    if r == 0:
-        c_zero = do("v", [], lambda: vec.memset(T.zero[:], 0))
-    do("v", [c_p], lambda: vec.tensor_scalar(T.ci4[:, 0:1], T.pci[:, 0:1], 4, None, OP.arith_shift_right))
-    do("v", [], lambda: vec.tensor_scalar(T.ci4[:, 1:2], T.pci[:, 0:1], 15, None, OP.bitwise_and))
-    do("v", [], lambda: vec.tensor_scalar(T.ci4[:, 2:3], T.pci[:, 0:1], 1, 7, OP.arith_shift_right, OP.bitwise_and))
-    x = do("v", [], lambda: vec.tensor_scalar(T.ci4[:, 3:4], T.pci[:, 0:1], 1, None, OP.bitwise_and))
-    c_cf = do("v", [x], lambda: vec.tensor_copy(T.cf4[:], T.ci4[:]))
-    c_bo = do("v", [c_cf, c_ig], lambda: vec.tensor_scalar(T.bo[:], T.igf[:], T.cf4[:, 0:1], None, OP.is_equal))
-    c_bom = do("v", [c_bo], lambda: vec.tensor_scalar(T.bom[:], T.bo[:], -4.0, None, OP.mult))
-    x = do("v", [], lambda: vec.tensor_scalar(T.cols[:, 2:3], T.cf4[:, 3:4], 100.0, T.cf4[:, 2:3], OP.mult, OP.add))
-    c_k0 = do("v", [], lambda: vec.tensor_scalar(T.cols[:, 0:1], T.cf4[:, 3:4], -100.0, T.cf4[:, 2:3], OP.mult, OP.add))
-    c_k1 = do("v", [x], lambda: vec.tensor_scalar(T.cols[:, 1:2], T.cols[:, 2:3], -100.0, None, OP.add))
-    c_mask = do("v", [c_row], lambda: vec.tensor_scalar(T.mask[:], T.rowf[:, 0:16], T.cf4[:, 1:2], None, OP.is_equal))
-    do("t", [c_bom, c_one], lambda: g.tensor.matmul(T.px[:, 0:128], T.bo[:], T.bom[:], True, False))
-    m_sy = do("v", [l_sy], lambda: vec.tensor_scalar(T.syb[:], T.syr[:], 64.0, None, OP.add))
-    m_x = do("t", [m_sy], lambda: g.tensor.matmul(T.px[:, 0:128], T.one[:], T.syb[:], False, True))
-    m_ti = do("v", [l_nx], lambda: vec.tensor_scalar(T.ti[:], T.nxi[:], 511, None, OP.bitwise_and))
-    m_s0 = do("v", [m_x, c_k0], lambda: vec.tensor_scalar(T.sel[:, 0:128], T.px[:, 0:128], T.cols[:, 0:1], None, OP.is_equal))
-    m_s1 = do("v", [c_k1], lambda: vec.tensor_scalar(T.sel[:, 128:256], T.px[:, 0:128], T.cols[:, 1:2], None, OP.is_equal))
-    m_tb = do("v", [m_ti], lambda: vec.tensor_scalar(T.tb[:], T.ti[:], -256.0, None, OP.add))
+    c_zero = do("v", [], lambda: vec.memset(T.zero[:], 0)) if r == 0 else None
+    P1, CI, CF, CO = T.pci[:, 0:1], T.ci5, T.cf5, T.cols
+    ts([c_p], CI[:, 0:1], P1, 4, None, OP.arith_shift_right)
+    ts([], CI[:, 1:2], P1, 15, None, OP.bitwise_and)
+    ts([], CI[:, 2:3], P1, 1, 7, OP.arith_shift_right, OP.bitwise_and)
+    ts([], CI[:, 3:4], P1, 1, None, OP.bitwise_and)
+    x = ts([], CI[:, 4:5], P1, 4, 1, OP.arith_shift_right, OP.bitwise_and)
+    c_cf = do("v", [x], lambda: vec.tensor_copy(CF[:], CI[:]))
+    c_bo = ts([c_cf, c_ig], T.bo[:], T.igf[:], CF[:, 0:1], None, OP.is_equal)
+    x = ts([], CO[:, 2:3], CF[:, 3:4], 100.0, CF[:, 2:3], OP.mult, OP.add)
+    c_k0 = ts([], CO[:, 0:1], CF[:, 3:4], -100.0, CF[:, 2:3], OP.mult, OP.add)
+    c_bom = ts([c_bo], T.bom[:], T.bo[:], -4.0, None, OP.mult)
+    c_k1 = ts([x], CO[:, 1:2], CO[:, 2:3], -100.0, None, OP.add)
+    c_mask = ts([c_row], T.mask[:], T.rowf[:, 0:16], CF[:, 1:2], None, OP.is_equal)
+    if r > 0:
+        ne = do("v", [], lambda: vec.tensor_tensor(CO[:, 4:5], CF[:, 4:5], CF[:, 3:4], OP.not_equal))
+        gt = do("v", [], lambda: vec.tensor_tensor(CO[:, 5:6], CF[:, 3:4], CF[:, 4:5], OP.is_gt))
+        c_id = ts([c_pf], T.idn[:], T.rowf[:], T.pf[:], None, OP.is_equal) if r > 1 else None
+        k = ts([ne], CO[:, 6:7], CO[:, 4:5], 256.0, CF[:, 2:3], OP.mult, OP.add)
+        do("v", [], lambda: vec.memset(T.tq[:, 0:16], 0.0))
+        k = ts([k], CO[:, 7:8], CF[:, 4:5], 16.0, CO[:, 6:7], OP.mult, OP.add)
+        do("v", [], lambda: vec.memset(T.tq[:, 272:288], 0.0))
+        k = ts([k, gt], CO[:, 8:9], CO[:, 5:6], 32.0, CO[:, 7:8], OP.mult, OP.add)
+        c_k9 = ts([k], CO[:, 9:10], CO[:, 8:9], 8.0, None, OP.add)
+        for m in range(8 if r > 1 else 0):
+            c_im = do("s", [c_id, c_mask], lambda: act(T.idm[:, 128 * m:128 * m + 128], T.idn[:], AF.Copy,
+                                                       scale=T.mask[:, 2 * m + 1:2 * m + 2]))
+    do("t", [c_bom, c_one], lambda: mm(T.px[:, 0:128], T.bo[:], T.bom[:], True, False))
+    m_sy = ts([l_sy], T.syb[:], T.syr[:], 64.0, None, OP.add)
+    m_x = do("t", [m_sy], lambda: mm(T.px[:, 0:128], T.one[:], T.syb[:], False, True))
+    m_ti = ts([l_nx], T.ti[:], T.nxi[:], 511, None, OP.bitwise_and)
+    ts([m_x, c_k0], T.sel[:, 0:128], T.px[:, 0:128], CO[:, 0:1], None, OP.is_equal)
+    m_s1 = ts([c_k1], T.sel[:, 128:256], T.px[:, 0:128], CO[:, 1:2], None, OP.is_equal)
+    m_tb = ts([m_ti], T.tb[:], T.ti[:], -256.0, None, OP.add)
 
-    def window_ab(sel, tb, w, deps, bank_free):
-        a = do("t", deps + bank_free, lambda: g.tensor.matmul(T.pwa[:, 0:256], sel[:, 0:128], tb[:], True, True))
-        b = do("t", [], lambda: g.tensor.matmul(T.pwb[:, 0:256], sel[:, 128:256], tb[:], True, True))
-        va = do("v", [a], lambda: vec.tensor_scalar(w[:, 0:256], T.pwa[:, 0:256], 256.0, None, OP.add))
-        sb = do("s", [b], lambda: g.scalar.activation(w[:, 256:512], T.pwb[:, 0:256], AF.Identity, bias=256.0))
+    def window_ab(sel, tb, w, deps):
+        a = do("t", deps, lambda: mm(T.pwa[:, 0:256], sel[:, 0:128], tb[:], True, True))
+        b = do("t", [], lambda: mm(T.pwb[:, 0:256], sel[:, 128:256], tb[:], True, True))
+        va = do("v", [a], lambda: vec.tensor_copy(w[:, 0:256], T.pwa[:, 0:256]))
+        sb = do("s", [b], lambda: act(w[:, 256:512], T.pwb[:, 0:256], AF.Copy))
         return [va, sb]
 
     def window_s(sel, tb, w, deps):
-        do("t", deps, lambda: g.tensor.matmul(T.psw[:, 0:256], sel[:, 0:128], tb[:], True, True))
-        b = do("t", [], lambda: g.tensor.matmul(T.psw[:, 256:512], sel[:, 128:256], tb[:], True, True))
-        return [do("s", [b], lambda: g.scalar.activation(w[:], T.psw[:], AF.Identity, bias=256.0))]
+        do("t", deps, lambda: mm(T.psw[:, 0:256], sel[:, 0:128], tb[:], True, True))
+        b = do("t", [], lambda: mm(T.psw[:, 256:512], sel[:, 128:256], tb[:], True, True))
+        return [do("s", [b], lambda: act(w[:], T.psw[:], AF.Copy))]
 
     def code_table():
-        do("v", [l_em], lambda: vec.tensor_scalar(T.hi[:], T.emi[:], 18, None, OP.arith_shift_right))
-        a = do("v", [], lambda: vec.tensor_scalar(T.ci[:], T.nxi[:], 9, None, OP.arith_shift_right))
-        b = do("v", [], lambda: vec.tensor_scalar(T.ya[:], T.nxi[:], 2048.0, 64.0, OP.is_lt, OP.mult))
+        ts([l_em], T.hi[:], T.emi[:], 18, None, OP.arith_shift_right)
+        b = ts([], T.ya[:], T.nxi[:], 2048.0, 64.0, OP.is_lt, OP.mult)
+        ts([], T.ci[:], T.nxi[:], 9, None, OP.arith_shift_right)
         n = do("v", [b], lambda: vec.tensor_tensor(T.na[:], T.hi[:], T.ya[:], OP.min))
         z = do("v", [n], lambda: vec.tensor_tensor(T.za[:], T.ci[:], T.na[:], OP.subtract))
-        z = do("v", [z], lambda: vec.tensor_scalar(T.zb[:], T.za[:], -4.0, 262144.0, OP.add, OP.mult))
+        z = ts([z], T.zb[:], T.za[:], -4.0, 262144.0, OP.add, OP.mult)
         return do("v", [z], lambda: vec.tensor_tensor(T.ec[:], T.zb[:], T.emi[:], OP.add))
 
     def code_mm(sf, ec, deps):
-        do("t", deps, lambda: g.tensor.matmul(T.pew[:, 0:256], sf[:, 0:128], ec[:], True, True))
-        return do("t", [], lambda: g.tensor.matmul(T.pew[:, 256:512], sf[:, 128:256], ec[:], True, True))
+        do("t", deps, lambda: mm(T.pew[:, 0:256], sf[:, 0:128], ec[:], True, True))
+        return do("t", [], lambda: mm(T.pew[:, 256:512], sf[:, 128:256], ec[:], True, True))
 
-    def step(win, deps, tile, x0, j, reg):
-        k = (j - 1) % 16
-        nxt = reg + 16 + 18 * j
-        b = nxt - k
-        d = do("v", deps, lambda: vec.tensor_copy(T.tt[:, b:b + 16], win[:, 0:512].indirect(tile[:, x0:x0 + 1])))
-        return d, nxt
+    def code_window(sf, ec, w, deps):
+        b = code_mm(sf, ec, deps)
+        return do("s", [b], lambda: act(w[:], T.pew[:], AF.Copy))
 
-    def run(win, deps, tile, x0, reg, n, hook=None):
-        reads = []
-        d = None
-        for j in range(n):
-            reads.append((tile, x0, d if j else deps))
-            dd = deps if j == 0 else [d]
-            d, nx = step(win, dd, tile, x0, j, reg)
-            tile, x0 = T.tt, nx
-            if hook is not None and j == hook[0]:
-                hook[1]()
-        reads.append((tile, x0, d))
-        return reads
+    def float_sel(sf, sel, deps):
+        return do("s", deps, lambda: act(sf[:], sel[:], AF.Copy))
+
+    def lists():
+        sf = do("v", [l_sc], lambda: vec.tensor_copy(CO[:, 3:4], T.syc[:]))
+        ti = ts([l_tp], T.tpi[:], T.tp[:], 511, None, OP.bitwise_and)
+        d = ts([sf, c_mask], T.d16[:], T.mask[:], CO[:, 3:4], None, OP.mult)
+        am = do("t", [d], lambda: mm(T.py[:, 64:80], T.bo[:], T.d16[:], True, True))
+        tq = do("v", [ti], lambda: vec.tensor_copy(T.tq[:, 16:272], T.tpi[:]))
+        ts([am, c_k9], T.ot[:, 0:16:2], T.py[:, 64:80:2], 32.0, CO[:, 8:9], OP.mult, OP.add)
+        do("v", [tq], lambda: vec.transpose(T.tab[:, 0:256], T.tq[:, 16:272]))
+        o = ts([], T.ot[:, 1:16:2], T.py[:, 64:80:2], 32.0, CO[:, 9:10], OP.mult, OP.add)
+        tr = do("v", [tq], lambda: vec.transpose(T.tab[:, 256:544], T.tq[:, 0:288]))
+        return do("v", [tr, o], lambda: vec.tensor_copy(T.lt[:], T.tab[:].indirect(T.ot[:])))
+
+    def join(m, deps, qn):
+        out, src = T.cp[:, 512 * m:512 * m + 512], T.w[:].indirect(T.lt[:, 32 * m:32 * m + 32])
+        if qn == "v":
+            return do("v", deps, lambda: vec.tensor_copy(out, src))
+        return do("s", deps, lambda: act(out, src, AF.Copy))
+
+    on_s, on_v = [0, 1, 3, 4, 6], [2, 5, 7]
+
+    def gather(win, at, deps, k, col):
+        b = col - k
+        tile, x0, d = at
+        return (T.tt, col, ts([d] + deps, T.tt[:, b:b + 16], win.indirect(tile[:, x0:x0 + 1]), 256.0, None, OP.add))
+
+    def plain(at, w, deps, j, reg):
+        return gather(w[:], at, deps, (j - 1) % 16, reg + 16 + 18 * j)
 
     def follow(reads, ewin, edep, ee):
         last = None
         for j in range(16):
             tile, x0, d = reads[j]
-            dd = d if isinstance(d, list) else [d]
             b = 0 if j == 0 else 16 * j + 16
-            last = do("s", dd + [edep, c_mask], lambda: g.scalar.activation(
-                ee[:, b:b + 16], ewin[:, 0:512].indirect(tile[:, x0:x0 + 1]), AF.Copy, scale=T.mask[:, j:j + 1]))
+            last = do("s", [d, edep, c_mask], lambda: act(
+                ee[:, b:b + 16], ewin[:].indirect(tile[:, x0:x0 + 1]), AF.Copy, scale=T.mask[:, j:j + 1]))
         return last
+
+    def paired(at, pw, w, deps, reg, last_too, fill):
+        reads = []
+        for m in range(8):
+            k = (2 * m - 1) % 16
+            nxt = None
+            if m < 7 or last_too:
+                nxt = gather(pw(m), at, deps, k, reg + 16 + 18 * m)
+            reads += [at, gather(w[:], at, deps, k, reg + 196 + 18 * m)]
+            at = nxt
+            if m > 1 and fill:
+                fill.pop(0)()
+        return reads, at
+
+    def own_pair(m):
+        return T.cp[:, 512 * m:512 * m + 512]
+
+    gd, ed_, ydep = {}, {}, [None, 0]
 
     def total(ee, last, out):
         return do("v", [last], lambda: vec.tensor_reduce(out[:], ee[:, 15:271:17], AxisListType.X, OP.add))
 
-    cdep = {}
-    epdep = {}
-    ydep = [None, 0]
+    def gates(q, code, dep):
+        gd[q] = ts([dep, c_thr], T["g4%d" % q][:], T.thr[:], code[:], None, OP.is_le)
 
-    def counts(q, code, dep):
-        qi, cb = T["qi%d" % q], T["cb%d" % q]
-        a = do("v", [dep], lambda: vec.tensor_copy(qi[:, 0:1], code[:]))
-        b = do("v", [a], lambda: vec.tensor_scalar(qi[:, 1:2], qi[:, 0:1], 18, None, OP.arith_shift_right))
-        cdep[q] = do("v", [b], lambda: vec.tensor_scalar(cb[:], qi[:, 1:2], 0.0, 4.0, OP.min, OP.add))
+    def digits(q, code, dep):
+        qi, di, dp, ep = T["qi%d" % q], T["di%d" % q], T["dp%d" % q], T["ep%d" % q]
+        box = {}
 
-    def digits(q):
-        qi, cb, di = T["qi%d" % q], T["cb%d" % q], T["di%d" % q]
-        dp, g4, ep = T["dp%d" % q], T["g4%d" % q], T["ep%d" % q]
-        do("v", [], lambda: vec.tensor_scalar(di[:, 0:1], qi[:, 0:1], 63, None, OP.bitwise_and))
-        do("v", [], lambda: vec.tensor_scalar(di[:, 1:2], qi[:, 0:1], 6, 63, OP.arith_shift_right, OP.bitwise_and))
-        do("v", [], lambda: vec.tensor_scalar(di[:, 2:3], qi[:, 0:1], 12, 63, OP.arith_shift_right, OP.bitwise_and))
-        d = do("v", [], lambda: vec.tensor_scalar(di[:, 3:4], qi[:, 1:2], 63, None, OP.bitwise_and))
-        do("v", [cdep[q]], lambda: vec.tensor_scalar(g4[:], T.rowf[:, 0:4], cb[:], None, OP.is_lt))
-        x = do("v", [d], lambda: vec.tensor_scalar(dp[:], di[:], 1.0, None, OP.add))
-        epdep[q] = do("v", [x], lambda: vec.tensor_tensor(ep[:], dp[:], g4[:], OP.mult))
+        def d0():
+            box[0] = do("v", [dep], lambda: vec.tensor_copy(qi[:], code[:]))
 
-    banks = {}
+        def d1():
+            ts([box[0]], di[:, 0:1], qi[:], 63, None, OP.bitwise_and)
+            ts([], di[:, 1:2], qi[:], 6, 63, OP.arith_shift_right, OP.bitwise_and)
 
-    def base(q, bank, free):
-        banks[q] = bank
-        for n, b in enumerate(range(q)):
-            do("t", [cdep[b], c_bo] + free, lambda: g.tensor.matmul(bank[:, 0:1], T.bo[:], T["cb%d" % b][:], n == 0, False))
+        def d2():
+            ts([], di[:, 2:3], qi[:], 12, 63, OP.arith_shift_right, OP.bitwise_and)
+            box[1] = ts([], di[:, 3:4], qi[:], 18, 63, OP.arith_shift_right, OP.bitwise_and)
+
+        def d3():
+            box[2] = ts([box[1]], dp[:], di[:], 1.0, None, OP.add)
+
+        def d4():
+            ed_[q] = do("v", [box[2], gd[q]], lambda: vec.tensor_tensor(ep[:], dp[:], T["g4%d" % q][:], OP.mult))
+        return [d0, d1, d2, d3, d4]
+
+    def decode(q, code, dep):
+        return [lambda: gates(q, code, dep)] + digits(q, code, dep)
+
+    def play(fs):
+        for f in fs:
+            f()
+
+    banks = {0: T.pb, 1: T.pc, 2: T.px, 3: T.pb}
+    begun = {}
+    bdep = {}
+
+    def count(q, b, stop=False):
+        bank = banks[q]
+        for m in range(4):
+            bdep[q] = do("t", [gd[b], c_tri], lambda: mm(bank[:, 0:1], (T.tri if b == q else T.bo)[:], T["g4%d" % b][:, m:m + 1],
+                                                         q not in begun, stop and m == 3))
+            begun[q] = True
 
     def place(q, final):
-        bank = banks[q]
-        bd = do("t", [cdep[q], c_tri], lambda: g.tensor.matmul(bank[:, 0:1], T.tri[:], T["cb%d" % q][:], q == 0, True))
+        bank, oh, ep = banks[q], T["oh%d" % q], T["ep%d" % q]
         for m in range(4):
-            oh, ep = T["oh%d" % q], T["ep%d" % q]
-            o = do("v", [bd, epdep[q], c_io], lambda: vec.tensor_scalar(
-                oh[:, 32 * m:32 * m + 32], T.io4[:, 32 * m:32 * m + 32], bank[:, 0:1], ep[:, m:m + 1], OP.is_equal, OP.mult))
-            ydep[0] = do("t", [o, c_gi], lambda: g.tensor.matmul(
+            o = ts([bdep[q], ed_[q], c_io], oh[:, 32 * m:32 * m + 32], T.io4[:, 32 * m:32 * m + 32], bank[:, 0:1],
+                   ep[:, m:m + 1], OP.is_equal, OP.mult)
+            ydep[0] = do("t", [o, c_gi], lambda: mm(
                 T.py[0:8, 0:32], T.gind[:], oh[:, 32 * m:32 * m + 32], ydep[1] == 0, final and m == 3))
             ydep[1] += 1
 
     def late_constants():
-        a = do("v", [c_row, c_pf], lambda: vec.tensor_scalar(T.tri0[:], T.rowf[:], T.pf[:], None, OP.is_gt))
-        gi = do("v", [], lambda: vec.tensor_scalar(T.gind[:], T.rowf[:, 0:8], T.cf4[:, 0:1], None, OP.is_equal))
-        tr = do("v", [a], lambda: vec.tensor_tensor(T.tri[:], T.tri0[:], T.bo[:], OP.mult))
-        return tr, gi
-
-    S1A, S1B = [2, 3], [1]
-    G1, C0, C1, C2 = [2, 3], [2, 3, 1], [2, 3, 0], [3, 1]
-
-    wdep = window_ab(T.sel, T.tb, T.w, [m_s1, m_tb], [])
-    sfd = do("s", [m_s1], lambda: g.scalar.activation(T.self[:], T.sel[:], AF.Copy))
+        a = ts([c_row, c_pf], T.tri0[:], T.rowf[:], T.pf[:], None, OP.is_gt)
+        th = ts([], T.thr[:], T.rowf[:, 0:4], -3.0, 262144.0, OP.add, OP.mult)
+        gi = ts([], T.gind[:], T.rowf[:, 0:8], CF[:, 0:1], None, OP.is_equal)
+        return do("v", [a], lambda: vec.tensor_tensor(T.tri[:], T.tri0[:], T.bo[:], OP.mult)), gi, th
 
     if r == 0:
-        rd = run(T.w, wdep + [c_zero], T.zero, 0, 0, 16)
-        xs = rd[16][1]
-        send([rd[16][2]], S1A, "s1", T.tt[:, xs:xs + 2], "as1")
-        send([], S1B, "s1", T.tt[:, xs:xs + 2], "as1")
+        wdep = window_ab(T.sel, T.tb, T.w, [m_s1, m_tb])
+        at = (T.zero, 0, c_zero)
+        reads = []
+        for j in range(16):
+            reads.append(at)
+            at = plain(at, T.w, wdep, j, 0)
+        s1 = T.tt[:, at[1]:at[1] + 2]
+        send([at[2]], [2, 3], "s1", s1, "as1")
+        send([], [1], "s1", s1, "as1")
+        sfd = float_sel(T.self, T.sel, [m_s1])
         ecd = code_table()
-        c_tri, c_gi = late_constants()
-        em = code_mm(T.self, T.ec, [sfd, ecd])
-        ed = do("s", [em], lambda: g.scalar.activation(T.e[:], T.pew[:], AF.Copy))
-        last = follow(rd, T.e, ed, T.eea)
-        oc = total(T.eea, last, T.oc)
-        send([oc], C0, "rc0", T.oc[:], "arc0")
-        counts(0, T.oc, oc)
-        digits(0)
-        base(0, T.pb, [])
+        c_tri, c_gi, c_thr = late_constants()
+        ed = code_window(T.self, T.ec, T.e, [sfd, ecd])
+        oc = total(T.eea, follow(reads, T.e, ed, T.eea), T.oca)
+        send([oc], [2, 3, 1], "rc0", T.oca[:], "arc0")
+        play(decode(0, T.oca, oc))
+        count(0, 0, True)
         place(0, False)
-        counts(1, T.rc1, arrive(1, C1, "arc1"))
-        base(1, T.pc, [])
-        digits(1)
+        count(1, 0)
+        a1 = arrive(1, "arc1")
+        gates(1, T.rc1, a1)
+        count(1, 1, True)
+        play(digits(1, T.rc1, a1))
         place(1, True)
     elif r == 1:
-        send([m_s1], G1, "sel1", T.sel[:], "asel1")
-        send([m_tb], G1, "tb1", T.tb[:], "atb1")
+        wdep = window_ab(T.sel, T.tb, T.w, [m_s1, m_tb])
+        send(wdep, [2, 3], "w1", T.w[:], "aw1")
+        sfd = float_sel(T.self, T.sel, [m_s1])
+        ltd = lists()
+        cpd = {}
+        for m in on_s:
+            cpd[m] = join(m, wdep + [ltd], "s")
         ecd = code_table()
-        c_tri, c_gi = late_constants()
-        em = code_mm(T.self, T.ec, [sfd, ecd])
-        ed = do("s", [em], lambda: g.scalar.activation(T.e[:], T.pew[:], AF.Copy))
-        rd = run(T.w, wdep + [arrive(0, S1B, "as1")], T.s1, 0, 0, 15)
-        last = follow(rd, T.e, ed, T.eea)
-        oc = total(T.eea, last, T.oc)
-        send([oc], C1, "rc1", T.oc[:], "arc1")
-        counts(1, T.oc, oc)
-        digits(1)
-        counts(0, T.rc0, arrive(0, C0, "arc0"))
-        base(0, T.pb, [])
-        digits(0)
+        for m in on_v:
+            cpd[m] = join(m, wdep + [ltd], "v")
+        c_tri, c_gi, c_thr = late_constants()
+        ed = code_window(T.self, T.ec, T.e, [sfd, ecd])
+        axs = arrive(3, "aselx")
+        sfx = float_sel(T.selfx, T.selx, [axs])
+        wxd = window_s(T.selx, T.tbx, T.wx, [axs, arrive(3, "atbx")])
+        exm = code_mm(T.selfx, T.ecx, [sfx, arrive(3, "aecx"), ed])
+        at = (T.s1, 0, arrive(0, "as1"))
+        reads, at = paired(at, own_pair, T.w, wdep + [cpd[6], cpd[7]], 0, True, [])
+        last = follow(reads, T.e, ed, T.eea)
+        exd = do("s", [exm], lambda: act(T.ex[:], T.pew[:], AF.Copy))
+        reads = []
+        fill = []
+        for j in range(16):
+            reads.append(at)
+            if j < 15:
+                at = plain(at, T.wx, wxd, j, 360)
+            if j == 1:
+                oc = total(T.eea, last, T.oca)
+                send([oc], [2, 3, 0], "rc1", T.oca[:], "arc1")
+                fill = decode(1, T.oca, oc) + decode(0, T.rc0, arrive(0, "arc0"))
+            elif fill:
+                fill.pop(0)()
+        last = follow(reads, T.ex, exd, T.eeb)
+        play(fill)
+        count(0, 0, True)
+        count(1, 0)
+        count(1, 1, True)
+        count(2, 0)
+        count(2, 1)
         place(0, False)
-        base(1, T.pc, [])
         place(1, False)
-        base(2, T.px, [m_s1])
-        counts(2, T.rc2, arrive(2, C2, "arc2"))
-        digits(2)
+        oc = total(T.eeb, last, T.ocb)
+        gates(2, T.ocb, oc)
+        count(2, 2, True)
+        play(digits(2, T.ocb, oc))
         place(2, True)
     else:
         o = 5 - r
+        wdep = window_s(T.sel, T.tb, T.w, [m_s1, m_tb])
+        sfd = float_sel(T.self, T.sel, [m_s1])
         send([m_s1], [o], "selx", T.sel[:], "aselx")
         send([m_tb], [o], "tbx", T.tb[:], "atbx")
+        ltd = lists()
+        cpd = {}
+        for m in on_s:
+            cpd[m] = join(m, wdep + [ltd], "s")
         ecd = code_table()
-        if r == 3:
-            send([ecd], [2], "ecx", T.ec[:], "aecx")
-        c_tri, c_gi = late_constants()
-        a_sx, a_tx = arrive(o, [r], "aselx"), arrive(o, [r], "atbx")
-        a_s1, a_t1 = arrive(1, G1, "asel1"), arrive(1, G1, "atb1")
-        w1dep = window_ab(T.sel1, T.tb1, T.w1, [a_s1, a_t1], wdep)
-        wxdep = window_s(T.selx, T.tbx, T.wx, [a_sx, a_tx])
+        send([ecd], [o], "ecx", T.ec[:], "aecx")
+        for m in on_v:
+            cpd[m] = join(m, wdep + [ltd], "v")
+        for n, m in enumerate([0, 1, 3, 4, 2, 6, 5, 7]):
+            md = do("t", [cpd[m], c_im], lambda: mm(T.pwa[:], T.idm[:, 128 * m:128 * m + 128], own_pair(m), n == 0, n == 7))
         em = code_mm(T.self, T.ec, [sfd, ecd])
-        ed = do("s", [em], lambda: g.scalar.activation(T.e[:], T.pew[:], AF.Copy))
-        rd1 = run(T.w1, w1dep + [arrive(0, S1A, "as1")], T.s1, 0, 0, 16)
-        t2 = rd1[16]
-        wins = {r: (T.w, wdep), o: (T.wx, wxdep)}
-        rd2 = run(wins[2][0], wins[2][1] + [t2[2]], t2[0], t2[1], 320, 16)
-        t3 = rd2[16]
-        if r == 2:
-            last2 = follow(rd2, T.e, ed, T.eea)
-            box = []
+        cmd = do("v", [md], lambda: vec.tensor_copy(T.cpm[:], T.pwa[:]))
+        axs, axt, axe = arrive(o, "aselx"), arrive(o, "atbx"), arrive(o, "aecx")
+        if r == 3:
+            send([axs], [1], "selx", T.selx[:], "aselx")
+            send([axt], [1], "tbx", T.tbx[:], "atbx")
+        send([cmd], [o], "cpx", T.cpm[:], "acpx")
+        if r == 3:
+            send([axe], [1], "ecx", T.ecx[:], "aecx")
+        c_tri, c_gi, c_thr = late_constants()
+        ed = do("s", [em], lambda: act(T.e[:], T.pew[:], AF.Copy))
+        sfx = float_sel(T.selfx, T.selx, [axs])
+        wxd = window_s(T.selx, T.tbx, T.wx, [axs, axt])
+        exd = code_window(T.selfx, T.ecx, T.ex, [sfx, axe, ed])
 
-            def mid():
-                oc = total(T.eea, last2, T.oc)
-                send([oc], C2, "rc2", T.oc[:], "arc2")
-                box.append(oc)
-            rd3 = run(wins[3][0], wins[3][1] + [t3[2]], t3[0], t3[1], 640, 15, hook=(2, mid))
-            sfx = do("s", [], lambda: g.scalar.activation(T.selfx[:], T.selx[:], AF.Copy))
-            em = code_mm(T.selfx, T.ecx, [sfx, arrive(3, [2], "aecx"), ed])
-            exd = do("s", [em], lambda: g.scalar.activation(T.ex[:], T.pew[:], AF.Copy))
-            last3 = follow(rd3, T.ex, exd, T.eeb)
-            counts(2, T.oc, box[0])
-            digits(2)
-            counts(0, T.rc0, arrive(0, C0, "arc0"))
-            counts(1, T.rc1, arrive(1, C1, "arc1"))
-            base(1, T.pb, [])
-            digits(1)
+        at = (T.s1, 0, arrive(0, "as1"))
+        aw1 = [arrive(1, "aw1")]
+        for j in range(16):
+            at = plain(at, T.w1, aw1, j, 0)
+        runs = {r: (own_pair, T.w, wdep + [cpd[6], cpd[7]], T.e, ed),
+                o: (lambda m: T.cpx[:], T.wx, wxd + [arrive(o, "acpx")], T.ex, exd)}
+        pw, w, deps, e2, e2d = runs[2]
+        reads, at = paired(at, pw, w, deps, 320, True, [])
+        last = follow(reads, e2, e2d, T.eea)
+        box = {}
+        a0, a1 = arrive(0, "arc0"), arrive(1, "arc1")
+
+        def t2():
+            box[0] = total(T.eea, last, T.oca)
+
+        def t3():
+            box[1] = total(T.eeb, last3, T.ocb)
+        fill = [lambda: gates(0, T.rc0, a0), t2, lambda: gates(2, T.oca, box[0])] + digits(2, T.oca, None)
+        pw, w, deps, e3, e3d = runs[3]
+        reads, _x = paired(at, pw, w, deps, 680, False, fill)
+        last3 = follow(reads, e3, e3d, T.eeb)
+        gates(1, T.rc1, a1)
+        if r == 2:
+            count(1, 0)
+            count(1, 1, True)
+            fill += digits(1, T.rc1, a1)
+        count(2, 0)
+        count(2, 1)
+        count(3, 0)
+        count(3, 1)
+        count(2, 2, True)
+        count(3, 2)
+        todo = [t3, lambda: gates(3, T.ocb, box[1])] + digits(3, T.ocb, None)
+        while todo or fill:
+            play(todo[:1] + fill[:1])
+            todo, fill = todo[1:], fill[1:]
+        count(3, 3, True)
+        if r == 2:
             place(1, False)
-            base(2, T.pc, [])
-            place(2, False)
-            base(3, T.px, [m_s1])
-            oc3 = total(T.eeb, last3, T.oc3)
-            counts(3, T.oc3, oc3)
-            digits(3)
-            place(3, True)
-        else:
-            rd3 = run(wins[3][0], wins[3][1] + [t3[2]], t3[0], t3[1], 640, 15)
-            last3 = follow(rd3, T.e, ed, T.eea)
-            oc3 = total(T.eea, last3, T.oc3)
-            counts(3, T.oc3, oc3)
-            digits(3)
-            counts(0, T.rc0, arrive(0, C0, "arc0"))
-            counts(1, T.rc1, arrive(1, C1, "arc1"))
-            counts(2, T.rc2, arrive(2, C2, "arc2"))
-            base(2, T.pb, [])
-            base(3, T.pc, [])
-            digits(2)
-            place(2, False)
-            place(3, True)
-    yd = do("v", [ydep[0]], lambda: vec.tensor_scalar(T.ysb[:], T.py[0:8, 0:32], -1.0, None, OP.add))
+        place(2, False)
+        place(3, True)
+    yd = ts([ydep[0]], T.ysb[:], T.py[0:8, 0:32], -1.0, None, OP.add)
     dma("y", [yd], "st", T.y[:], T.ysb[:])
     for sn in list(cnt):
         if sn != "st":

@@ -21,24 +21,23 @@ SCRATCH = {
     "selx": ("sbuf", [128, 256], H), "tbx": ("sbuf", [128, 256], H), "ecx": ("sbuf", [128, 256], F),
     "w": ("sbuf", [128, 512], H), "w1": ("sbuf", [128, 512], H), "wx": ("sbuf", [128, 512], H),
     "e": ("sbuf", [128, 512], F), "ex": ("sbuf", [128, 512], F),
-    "cp": ("sbuf", [128, 4096], H), "cpm": ("sbuf", [128, 512], H), "cpx": ("sbuf", [128, 512], H),
+    "cp": ("sbuf", [128, 4096], H), "cpm": ("sbuf", [128, 512], H), "cpx": ("sbuf", [128, 512], H), "cp1": ("sbuf", [128, 512], H),
     "s1": ("sbuf", [128, 2], U), "zero": ("sbuf", [128, 2], U), "tt": ("sbuf", [128, 1080], U),
     "eea": ("sbuf", [128, 272], F), "eeb": ("sbuf", [128, 272], F),
     "rc0": ("sbuf", [128, 1], F), "rc1": ("sbuf", [128, 1], F),
-    "oca": ("sbuf", [128, 1], F), "ocb": ("sbuf", [128, 1], F), "ysb": ("sbuf", [8, 32], F),
+    "oca": ("sbuf", [128, 1], F), "ocb": ("sbuf", [128, 1], F), "ysb": ("sbuf", [8, 32], F), "neg": ("sbuf", [8, 32], F),
     "px": ("psum", [128, 512], F), "pwa": ("psum", [128, 512], F), "pwb": ("psum", [128, 512], F),
-    "psw": ("psum", [128, 512], F), "pew": ("psum", [128, 512], F), "pb": ("psum", [128, 512], F),
+    "pcm": ("psum", [128, 512], F), "pew": ("psum", [128, 512], F), "pb": ("psum", [128, 512], F),
     "pc": ("psum", [128, 512], F), "py": ("psum", [128, 512], F),
 }
 for _q in range(4):
     SCRATCH["qi%d" % _q] = ("sbuf", [128, 1], I)
     SCRATCH["di%d" % _q] = ("sbuf", [128, 4], I)
-    SCRATCH["dp%d" % _q] = ("sbuf", [128, 4], F)
     SCRATCH["g4%d" % _q] = ("sbuf", [128, 4], H)
     SCRATCH["ep%d" % _q] = ("sbuf", [128, 4], F)
     SCRATCH["oh%d" % _q] = ("sbuf", [128, 128], H)
 SEMAPHORES = ["v", "s", "t", "p", "lnx", "lsy", "lsc", "ltp", "lem", "st", "loc",
-              "as1", "aw1", "aselx", "atbx", "aecx", "acpx", "arc0", "arc1"]
+              "as1", "aw1", "acp1", "aselx", "atbx", "aecx", "acpx", "arc0", "arc1"]
 OP = AluOpType
 AF = ActivationFunctionType
 
@@ -132,23 +131,25 @@ def rank_program(g, core, T, topo):
     if r > 0:
         ne = do("v", [], lambda: vec.tensor_tensor(CO[:, 4:5], CF[:, 4:5], CF[:, 3:4], OP.not_equal))
         gt = do("v", [], lambda: vec.tensor_tensor(CO[:, 5:6], CF[:, 3:4], CF[:, 4:5], OP.is_gt))
-        c_id = ts([c_pf], T.idn[:], T.rowf[:], T.pf[:], None, OP.is_equal) if r > 1 else None
+        c_id = ts([c_pf], T.idn[:], T.rowf[:], T.pf[:], None, OP.is_equal)
         k = ts([ne], CO[:, 6:7], CO[:, 4:5], 256.0, CF[:, 2:3], OP.mult, OP.add)
         do("v", [], lambda: vec.memset(T.tq[:, 0:16], 0.0))
         k = ts([k], CO[:, 7:8], CF[:, 4:5], 16.0, CO[:, 6:7], OP.mult, OP.add)
         do("v", [], lambda: vec.memset(T.tq[:, 272:288], 0.0))
         k = ts([k, gt], CO[:, 8:9], CO[:, 5:6], 32.0, CO[:, 7:8], OP.mult, OP.add)
         c_k9 = ts([k], CO[:, 9:10], CO[:, 8:9], 8.0, None, OP.add)
-        for m in range(8 if r > 1 else 0):
+        for m in range(4 if r == 1 else 0, 8):
             c_im = do("s", [c_id, c_mask], lambda: act(T.idm[:, 128 * m:128 * m + 128], T.idn[:], AF.Copy,
                                                        scale=T.mask[:, 2 * m + 1:2 * m + 2]))
     do("t", [c_bom, c_one], lambda: mm(T.px[:, 0:128], T.bo[:], T.bom[:], True, False))
     m_sy = ts([l_sy], T.syb[:], T.syr[:], 64.0, None, OP.add)
     m_x = do("t", [m_sy], lambda: mm(T.px[:, 0:128], T.one[:], T.syb[:], False, True))
-    m_ti = ts([l_nx], T.ti[:], T.nxi[:], 511, None, OP.bitwise_and)
     ts([m_x, c_k0], T.sel[:, 0:128], T.px[:, 0:128], CO[:, 0:1], None, OP.is_equal)
+    m_ta = ts([l_nx], T.ti[:, 0:128], T.nxi[:, 0:128], 511, None, OP.bitwise_and)
+    m_ti = ts([], T.ti[:, 128:256], T.nxi[:, 128:256], 511, None, OP.bitwise_and)
     m_s1 = ts([c_k1], T.sel[:, 128:256], T.px[:, 0:128], CO[:, 1:2], None, OP.is_equal)
-    m_tb = ts([m_ti], T.tb[:], T.ti[:], -256.0, None, OP.add)
+    ts([m_ta], T.tb[:, 0:128], T.ti[:, 0:128], -256.0, None, OP.add)
+    m_tb = ts([m_ti], T.tb[:, 128:256], T.ti[:, 128:256], -256.0, None, OP.add)
 
     def window_ab(sel, tb, w, deps):
         a = do("t", deps, lambda: mm(T.pwa[:, 0:256], sel[:, 0:128], tb[:], True, True))
@@ -157,10 +158,12 @@ def rank_program(g, core, T, topo):
         sb = do("s", [b], lambda: act(w[:, 256:512], T.pwb[:, 0:256], AF.Copy))
         return [va, sb]
 
-    def window_s(sel, tb, w, deps):
-        do("t", deps, lambda: mm(T.psw[:, 0:256], sel[:, 0:128], tb[:], True, True))
-        b = do("t", [], lambda: mm(T.psw[:, 256:512], sel[:, 128:256], tb[:], True, True))
-        return [do("s", [b], lambda: act(w[:], T.psw[:], AF.Copy))]
+    def window_mm(sel, tb, deps):
+        do("t", deps, lambda: mm(T.pwa[:, 0:256], sel[:, 0:128], tb[:], True, True))
+        return do("t", [], lambda: mm(T.pwa[:, 256:512], sel[:, 128:256], tb[:], True, True))
+
+    def window_out(w, d):
+        return [do("s", [d], lambda: act(w[:], T.pwa[:], AF.Copy))]
 
     def code_table():
         ts([l_em], T.hi[:], T.emi[:], 18, None, OP.arith_shift_right)
@@ -175,9 +178,8 @@ def rank_program(g, core, T, topo):
         do("t", deps, lambda: mm(T.pew[:, 0:256], sf[:, 0:128], ec[:], True, True))
         return do("t", [], lambda: mm(T.pew[:, 256:512], sf[:, 128:256], ec[:], True, True))
 
-    def code_window(sf, ec, w, deps):
-        b = code_mm(sf, ec, deps)
-        return do("s", [b], lambda: act(w[:], T.pew[:], AF.Copy))
+    def code_out(w, d):
+        return do("s", [d], lambda: act(w[:], T.pew[:], AF.Copy))
 
     def float_sel(sf, sel, deps):
         return do("s", deps, lambda: act(sf[:], sel[:], AF.Copy))
@@ -194,13 +196,20 @@ def rank_program(g, core, T, topo):
         tr = do("v", [tq], lambda: vec.transpose(T.tab[:, 256:544], T.tq[:, 0:288]))
         return do("v", [tr, o], lambda: vec.tensor_copy(T.lt[:], T.tab[:].indirect(T.ot[:])))
 
+    def own_pair(m):
+        return T.cp[:, 512 * m:512 * m + 512]
+
     def join(m, deps, qn):
-        out, src = T.cp[:, 512 * m:512 * m + 512], T.w[:].indirect(T.lt[:, 32 * m:32 * m + 32])
+        out, src = own_pair(m), T.w[:].indirect(T.lt[:, 32 * m:32 * m + 32])
         if qn == "v":
             return do("v", deps, lambda: vec.tensor_copy(out, src))
         return do("s", deps, lambda: act(out, src, AF.Copy))
 
-    on_s, on_v = [0, 1, 3, 4, 6], [2, 5, 7]
+    def merge(cpd, order):
+        for n, m in enumerate(order):
+            d = do("t", [cpd[m], c_im], lambda: mm(T.pcm[:], T.idm[:, 128 * m:128 * m + 128], own_pair(m),
+                                                   n == 0, n == len(order) - 1))
+        return do("s", [d], lambda: act(T.cpm[:], T.pcm[:], AF.Copy))
 
     def gather(win, at, deps, k, col):
         b = col - k
@@ -210,9 +219,9 @@ def rank_program(g, core, T, topo):
     def plain(at, w, deps, j, reg):
         return gather(w[:], at, deps, (j - 1) % 16, reg + 16 + 18 * j)
 
-    def follow(reads, ewin, edep, ee):
+    def follow(reads, ewin, edep, ee, first=0, end=16):
         last = None
-        for j in range(16):
+        for j in range(first, end):
             tile, x0, d = reads[j]
             b = 0 if j == 0 else 16 * j + 16
             last = do("s", [d, edep, c_mask], lambda: act(
@@ -232,9 +241,6 @@ def rank_program(g, core, T, topo):
                 fill.pop(0)()
         return reads, at
 
-    def own_pair(m):
-        return T.cp[:, 512 * m:512 * m + 512]
-
     gd, ed_, ydep = {}, {}, [None, 0]
 
     def total(ee, last, out):
@@ -244,7 +250,7 @@ def rank_program(g, core, T, topo):
         gd[q] = ts([dep, c_thr], T["g4%d" % q][:], T.thr[:], code[:], None, OP.is_le)
 
     def digits(q, code, dep):
-        qi, di, dp, ep = T["qi%d" % q], T["di%d" % q], T["dp%d" % q], T["ep%d" % q]
+        qi, di, ep = T["qi%d" % q], T["di%d" % q], T["ep%d" % q]
         box = {}
 
         def d0():
@@ -259,11 +265,8 @@ def rank_program(g, core, T, topo):
             box[1] = ts([], di[:, 3:4], qi[:], 18, 63, OP.arith_shift_right, OP.bitwise_and)
 
         def d3():
-            box[2] = ts([box[1]], dp[:], di[:], 1.0, None, OP.add)
-
-        def d4():
-            ed_[q] = do("v", [box[2], gd[q]], lambda: vec.tensor_tensor(ep[:], dp[:], T["g4%d" % q][:], OP.mult))
-        return [d0, d1, d2, d3, d4]
+            ed_[q] = do("v", [box[1], gd[q]], lambda: vec.tensor_tensor(ep[:], di[:], T["g4%d" % q][:], OP.mult))
+        return [d0, d1, d2, d3]
 
     def decode(q, code, dep):
         return [lambda: gates(q, code, dep)] + digits(q, code, dep)
@@ -285,12 +288,14 @@ def rank_program(g, core, T, topo):
 
     def place(q, final):
         bank, oh, ep = banks[q], T["oh%d" % q], T["ep%d" % q]
-        for m in range(4):
+
+        def one(m):
             o = ts([bdep[q], ed_[q], c_io], oh[:, 32 * m:32 * m + 32], T.io4[:, 32 * m:32 * m + 32], bank[:, 0:1],
                    ep[:, m:m + 1], OP.is_equal, OP.mult)
             ydep[0] = do("t", [o, c_gi], lambda: mm(
                 T.py[0:8, 0:32], T.gind[:], oh[:, 32 * m:32 * m + 32], ydep[1] == 0, final and m == 3))
             ydep[1] += 1
+        return [lambda: one(0), lambda: one(1), lambda: one(2), lambda: one(3)]
 
     def late_constants():
         a = ts([c_row, c_pf], T.tri0[:], T.rowf[:], T.pf[:], None, OP.is_gt)
@@ -311,39 +316,45 @@ def rank_program(g, core, T, topo):
         sfd = float_sel(T.self, T.sel, [m_s1])
         ecd = code_table()
         c_tri, c_gi, c_thr = late_constants()
-        ed = code_window(T.self, T.ec, T.e, [sfd, ecd])
+        ed = code_out(T.e, code_mm(T.self, T.ec, [sfd, ecd]))
         oc = total(T.eea, follow(reads, T.e, ed, T.eea), T.oca)
         send([oc], [2, 3, 1], "rc0", T.oca[:], "arc0")
         play(decode(0, T.oca, oc))
         count(0, 0, True)
-        place(0, False)
+        play(place(0, False))
         count(1, 0)
         a1 = arrive(1, "arc1")
         gates(1, T.rc1, a1)
         count(1, 1, True)
         play(digits(1, T.rc1, a1))
-        place(1, True)
+        play(place(1, True))
     elif r == 1:
         wdep = window_ab(T.sel, T.tb, T.w, [m_s1, m_tb])
         send(wdep, [2, 3], "w1", T.w[:], "aw1")
         sfd = float_sel(T.self, T.sel, [m_s1])
         ltd = lists()
         cpd = {}
-        for m in on_s:
+        for m in (4, 5, 6, 7):
+            cpd[m] = join(m, wdep + [ltd], "v" if m % 2 else "s")
+        cmd = merge(cpd, [4, 5, 6, 7])
+        send([cmd], [2, 3], "cp1", T.cpm[:], "acp1")
+        for m in (0, 1):
             cpd[m] = join(m, wdep + [ltd], "s")
         ecd = code_table()
-        for m in on_v:
+        for m in (2, 3):
             cpd[m] = join(m, wdep + [ltd], "v")
         c_tri, c_gi, c_thr = late_constants()
-        ed = code_window(T.self, T.ec, T.e, [sfd, ecd])
+        ed = code_out(T.e, code_mm(T.self, T.ec, [sfd, ecd]))
         axs = arrive(3, "aselx")
         sfx = float_sel(T.selfx, T.selx, [axs])
-        wxd = window_s(T.selx, T.tbx, T.wx, [axs, arrive(3, "atbx")])
+        wxm = window_mm(T.selx, T.tbx, wdep + [axs, arrive(3, "atbx")])
         exm = code_mm(T.selfx, T.ecx, [sfx, arrive(3, "aecx"), ed])
         at = (T.s1, 0, arrive(0, "as1"))
-        reads, at = paired(at, own_pair, T.w, wdep + [cpd[6], cpd[7]], 0, True, [])
-        last = follow(reads, T.e, ed, T.eea)
-        exd = do("s", [exm], lambda: act(T.ex[:], T.pew[:], AF.Copy))
+        reads, at = paired(at, own_pair, T.w, wdep + list(cpd.values()), 0, True, [])
+        last = follow(reads, T.e, ed, T.eea, 0, 8)
+        wxd = window_out(T.wx, wxm)
+        last = follow(reads, T.e, ed, T.eea, 8, 16)
+        exd = code_out(T.ex, exm)
         reads = []
         fill = []
         for j in range(16):
@@ -363,53 +374,54 @@ def rank_program(g, core, T, topo):
         count(1, 1, True)
         count(2, 0)
         count(2, 1)
-        place(0, False)
-        place(1, False)
+        play(place(0, False))
+        play(place(1, False))
         oc = total(T.eeb, last, T.ocb)
         gates(2, T.ocb, oc)
         count(2, 2, True)
         play(digits(2, T.ocb, oc))
-        place(2, True)
+        play(place(2, True))
     else:
         o = 5 - r
-        wdep = window_s(T.sel, T.tb, T.w, [m_s1, m_tb])
+        wdep = window_out(T.w, window_mm(T.sel, T.tb, [m_s1, m_tb]))
         sfd = float_sel(T.self, T.sel, [m_s1])
         send([m_s1], [o], "selx", T.sel[:], "aselx")
         send([m_tb], [o], "tbx", T.tb[:], "atbx")
         ltd = lists()
         cpd = {}
-        for m in on_s:
+        for m in (0, 1, 2, 4, 5, 6):
             cpd[m] = join(m, wdep + [ltd], "s")
         ecd = code_table()
         send([ecd], [o], "ecx", T.ec[:], "aecx")
-        for m in on_v:
+        for m in (3, 7):
             cpd[m] = join(m, wdep + [ltd], "v")
-        for n, m in enumerate([0, 1, 3, 4, 2, 6, 5, 7]):
-            md = do("t", [cpd[m], c_im], lambda: mm(T.pwa[:], T.idm[:, 128 * m:128 * m + 128], own_pair(m), n == 0, n == 7))
-        em = code_mm(T.self, T.ec, [sfd, ecd])
-        cmd = do("v", [md], lambda: vec.tensor_copy(T.cpm[:], T.pwa[:]))
+        cmd = merge(cpd, [0, 1, 2, 3, 4, 5, 7, 6])
         axs, axt, axe = arrive(o, "aselx"), arrive(o, "atbx"), arrive(o, "aecx")
         if r == 3:
             send([axs], [1], "selx", T.selx[:], "aselx")
             send([axt], [1], "tbx", T.tbx[:], "atbx")
-        send([cmd], [o], "cpx", T.cpm[:], "acpx")
-        if r == 3:
             send([axe], [1], "ecx", T.ecx[:], "aecx")
+        send([cmd], [o], "cpx", T.cpm[:], "acpx")
         c_tri, c_gi, c_thr = late_constants()
-        ed = do("s", [em], lambda: act(T.e[:], T.pew[:], AF.Copy))
         sfx = float_sel(T.selfx, T.selx, [axs])
-        wxd = window_s(T.selx, T.tbx, T.wx, [axs, axt])
-        exd = code_window(T.selfx, T.ecx, T.ex, [sfx, axe, ed])
+        wxd = window_out(T.wx, window_mm(T.selx, T.tbx, wdep + [axs, axt]))
+        codes = {r: (T.self, T.ec, [sfd, ecd], T.e), o: (T.selfx, T.ecx, [sfx, axe], T.ex)}
+        e2, e3 = codes[2][3], codes[3][3]
+        e2d = code_out(e2, code_mm(codes[2][0], codes[2][1], codes[2][2]))
+        m3 = code_mm(codes[3][0], codes[3][1], codes[3][2] + [e2d])
 
         at = (T.s1, 0, arrive(0, "as1"))
-        aw1 = [arrive(1, "aw1")]
-        for j in range(16):
+        aw1, acp1 = [arrive(1, "aw1")], [arrive(1, "acp1")]
+        for j in range(8):
             at = plain(at, T.w1, aw1, j, 0)
-        runs = {r: (own_pair, T.w, wdep + [cpd[6], cpd[7]], T.e, ed),
-                o: (lambda m: T.cpx[:], T.wx, wxd + [arrive(o, "acpx")], T.ex, exd)}
-        pw, w, deps, e2, e2d = runs[2]
+        for m in range(4, 8):
+            at = gather(T.cp1[:], at, acp1, 2 * m - 1, 16 + 36 * m)
+        runs = {r: (own_pair, T.w, wdep + list(cpd.values())),
+                o: (lambda m: T.cpx[:], T.wx, wxd + [arrive(o, "acpx")])}
+        pw, w, deps = runs[2]
         reads, at = paired(at, pw, w, deps, 320, True, [])
         last = follow(reads, e2, e2d, T.eea)
+        e3d = code_out(e3, m3)
         box = {}
         a0, a1 = arrive(0, "arc0"), arrive(1, "arc1")
 
@@ -419,30 +431,42 @@ def rank_program(g, core, T, topo):
         def t3():
             box[1] = total(T.eeb, last3, T.ocb)
         fill = [lambda: gates(0, T.rc0, a0), t2, lambda: gates(2, T.oca, box[0])] + digits(2, T.oca, None)
-        pw, w, deps, e3, e3d = runs[3]
+        pw, w, deps = runs[3]
         reads, _x = paired(at, pw, w, deps, 680, False, fill)
         last3 = follow(reads, e3, e3d, T.eeb)
-        gates(1, T.rc1, a1)
         if r == 2:
             count(1, 0)
+        count(2, 0)
+        count(2, 2)
+        count(3, 0)
+        count(3, 2)
+        gates(1, T.rc1, a1)
+        if r == 2:
             count(1, 1, True)
             fill += digits(1, T.rc1, a1)
-        count(2, 0)
-        count(2, 1)
-        count(3, 0)
+        count(2, 1, True)
         count(3, 1)
-        count(2, 2, True)
-        count(3, 2)
         todo = [t3, lambda: gates(3, T.ocb, box[1])] + digits(3, T.ocb, None)
-        while todo or fill:
-            play(todo[:1] + fill[:1])
-            todo, fill = todo[1:], fill[1:]
-        count(3, 3, True)
         if r == 2:
-            place(1, False)
-        place(2, False)
-        place(3, True)
-    yd = ts([ydep[0]], T.ysb[:], T.py[0:8, 0:32], -1.0, None, OP.add)
+            fill += place(1, False)
+        fill += place(2, False)
+        for n in range(len(todo)):
+            play(todo[n:n + 1] + fill[n:n + 1])
+            if n == 1:
+                count(3, 3, True)
+        play(fill[len(todo):])
+        if r == 3:
+            for b in range(4):
+                for m in range(4):
+                    zd = do("t", [gd[b], e3d], lambda: mm(T.pew[0:8, 0:1], T.gind[:], T["g4%d" % b][:, m:m + 1],
+                                                          b == 0 and m == 0, b == 3 and m == 3))
+        play(place(3, True))
+        if r == 3:
+            nd = ts([zd, c_io], T.neg[:], T.io4[0:8, 0:32], T.pew[0:8, 0:1], -1.0, OP.is_ge, OP.mult)
+    if r == 3:
+        yd = do("v", [ydep[0], nd], lambda: vec.tensor_tensor(T.ysb[:], T.py[0:8, 0:32], T.neg[:], OP.add))
+    else:
+        yd = do("v", [ydep[0]], lambda: vec.tensor_copy(T.ysb[:], T.py[0:8, 0:32]))
     dma("y", [yd], "st", T.y[:], T.ysb[:])
     for sn in list(cnt):
         if sn != "st":

@@ -6,25 +6,24 @@ F, H, I, U = "float32", "bfloat16", "int32", "uint16"
 SCRATCH = {
     "nxi": ("sbuf", [128, 256], I), "emi": ("sbuf", [128, 256], I), "syr": ("sbuf", [1, 128], I),
     "syb": ("sbuf", [1, 128], H), "one": ("sbuf", [1, 128], H), "syc": ("sbuf", [128, 1], I),
+    "evr": ("sbuf", [1, 128], F), "evh": ("sbuf", [1, 128], H), "evl": ("sbuf", [1, 128], H), "ramp": ("sbuf", [1, 512], H),
     "pci": ("sbuf", [128, 2], I), "pf": ("sbuf", [128, 1], F), "igf": ("sbuf", [128, 128], F),
     "rowf": ("sbuf", [128, 128], F), "io4": ("sbuf", [128, 128], F),
     "ci5": ("sbuf", [128, 5], I), "cf5": ("sbuf", [128, 5], F), "cols": ("sbuf", [128, 12], F),
-    "bo": ("sbuf", [128, 128], H), "bom": ("sbuf", [128, 128], H), "tri": ("sbuf", [128, 128], H),
-    "tri0": ("sbuf", [128, 128], H), "mask": ("sbuf", [128, 16], F), "gind": ("sbuf", [128, 8], H), "thr": ("sbuf", [128, 4], F),
-    "idn": ("sbuf", [128, 128], H), "idm": ("sbuf", [128, 1024], H),
-    "ti": ("sbuf", [128, 256], I), "sel": ("sbuf", [128, 256], H), "tb": ("sbuf", [128, 256], H),
-    "hi": ("sbuf", [128, 256], I), "ci": ("sbuf", [128, 256], I), "ya": ("sbuf", [128, 256], F),
-    "na": ("sbuf", [128, 256], F), "za": ("sbuf", [128, 256], F), "zb": ("sbuf", [128, 256], F),
-    "ec": ("sbuf", [128, 256], F), "self": ("sbuf", [128, 256], F), "selfx": ("sbuf", [128, 256], F),
+    "bo": ("sbuf", [128, 128], H), "tri": ("sbuf", [128, 128], H), "idn": ("sbuf", [128, 128], H),
+    "mask": ("sbuf", [128, 16], F), "pm": ("sbuf", [128, 8], F), "gind": ("sbuf", [128, 8], H), "thr": ("sbuf", [128, 4], F),
+    "ti": ("sbuf", [128, 256], I), "sel": ("sbuf", [128, 256], H), "selo": ("sbuf", [128, 256], H), "tb": ("sbuf", [128, 256], H),
+    "hi": ("sbuf", [128, 256], I), "ci": ("sbuf", [128, 256], I), "za": ("sbuf", [128, 256], H), "emf": ("sbuf", [128, 256], F),
+    "self": ("sbuf", [128, 256], F), "selc": ("sbuf", [128, 256], H), "selfx": ("sbuf", [128, 256], F),
+    "selx": ("sbuf", [128, 256], H), "emx": ("sbuf", [128, 256], F), "zax": ("sbuf", [128, 256], H),
     "tp": ("sbuf", [128, 256], I), "tpi": ("sbuf", [128, 256], I), "tq": ("sbuf", [128, 288], F), "tab": ("sbuf", [128, 544], F),
-    "d16": ("sbuf", [128, 16], H), "ot": ("sbuf", [128, 16], U), "lt": ("sbuf", [128, 256], U),
-    "selx": ("sbuf", [128, 256], H), "tbx": ("sbuf", [128, 256], H), "ecx": ("sbuf", [128, 256], F),
+    "d16": ("sbuf", [128, 16], H), "ot": ("sbuf", [128, 32], U), "lt": ("sbuf", [128, 512], U),
     "w": ("sbuf", [128, 512], H), "w1": ("sbuf", [128, 512], H), "wx": ("sbuf", [128, 512], H),
     "e": ("sbuf", [128, 512], F), "ex": ("sbuf", [128, 512], F),
     "cp": ("sbuf", [128, 4096], H), "cpm": ("sbuf", [128, 512], H), "cpx": ("sbuf", [128, 512], H), "cp1": ("sbuf", [128, 512], H),
     "s1": ("sbuf", [128, 2], U), "zero": ("sbuf", [128, 2], U), "tt": ("sbuf", [128, 1080], U),
-    "eea": ("sbuf", [128, 272], F), "eeb": ("sbuf", [128, 272], F),
-    "rc0": ("sbuf", [128, 1], F), "rc1": ("sbuf", [128, 1], F),
+    "eea": ("sbuf", [128, 272], F), "eeb": ("sbuf", [128, 272], F), "pos": ("sbuf", [128, 4], F), "zed": ("sbuf", [8, 1], F),
+    "rc0": ("sbuf", [128, 1], F), "rc1": ("sbuf", [128, 1], F), "rc2": ("sbuf", [128, 1], F),
     "oca": ("sbuf", [128, 1], F), "ocb": ("sbuf", [128, 1], F), "ysb": ("sbuf", [8, 32], F), "neg": ("sbuf", [8, 32], F),
     "px": ("psum", [128, 512], F), "pwa": ("psum", [128, 512], F), "pwb": ("psum", [128, 512], F),
     "pcm": ("psum", [128, 512], F), "pew": ("psum", [128, 512], F), "pb": ("psum", [128, 512], F),
@@ -37,9 +36,12 @@ for _q in range(4):
     SCRATCH["ep%d" % _q] = ("sbuf", [128, 4], F)
     SCRATCH["oh%d" % _q] = ("sbuf", [128, 128], H)
 SEMAPHORES = ["v", "s", "t", "p", "lnx", "lsy", "lsc", "ltp", "lem", "st", "loc",
-              "as1", "aw1", "acp1", "aselx", "atbx", "aecx", "acpx", "arc0", "arc1"]
+              "as1", "aw1", "acp1", "awx", "aselx", "aemx", "azax", "acpx", "arc0", "arc1", "arc2"]
 OP = AluOpType
 AF = ActivationFunctionType
+FIRST = {2: 1, 3: 0}
+FOURS = (8, 12)
+CODE = 262144.0
 
 
 def rank_program(g, core, T, topo):
@@ -50,6 +52,7 @@ def rank_program(g, core, T, topo):
     cnt = {}
     seen = {}
     vec, act, mm = g.vector, g.scalar.activation, g.tensor.matmul
+    first = FIRST.get(r, 8)
 
     def waits(qn, deps):
         need = {}
@@ -83,21 +86,35 @@ def rank_program(g, core, T, topo):
                 m &= topo.mask(T.cores[src], c)
         return m
 
-    def send(deps, dsts, name_out, src, sn):
-        waits("p", deps)
-        m = fan(r)
-        ids = []
-        for d in dsts:
-            rid, pid, _ = topo.addr(T.cores[d])
-            ids.append(DstId(rid=rid, pnc=pid))
-        g.remote_dma_fused([RemoteDMATransfer(dst_ids=ids, dma_engine_mask=m, remote_sem=T.sem[sn], srcs=[src],
-                                              dsts=[T[name_out][:] for _ in dsts], alu_op=0)],
-                           local_sem=T.sem.loc)
-        cnt["loc"] = cnt.get("loc", 0) + bin(m).count("1")
+    def inside(src, dst):
+        if topo.chip(T.cores[src]) != topo.chip(T.cores[dst]):
+            return 0
+        return topo.mask(T.cores[src], T.cores[dst]) & ~fan(src)
 
-    def arrive(src, sn):
-        cnt[sn] = bin(fan(src)).count("1")
+    def send(deps, dsts, name_out, src, sn, apart=False):
+        waits("p", deps)
+        lanes = {}
+        for d in dsts:
+            m = (inside(r, d) if apart else 0) or fan(r)
+            lanes[m] = lanes.get(m, []) + [d]
+        trs = []
+        for m in lanes:
+            ids = []
+            for d in lanes[m]:
+                rid, pid, _ = topo.addr(T.cores[d])
+                ids.append(DstId(rid=rid, pnc=pid))
+            trs.append(RemoteDMATransfer(dst_ids=ids, dma_engine_mask=m, remote_sem=T.sem[sn], srcs=[src],
+                                         dsts=[T[name_out][:] for _ in ids], alu_op=0))
+            cnt["loc"] = cnt.get("loc", 0) + bin(m).count("1")
+        g.remote_dma_fused(trs, local_sem=T.sem.loc)
+
+    def arrive(src, sn, apart=False):
+        cnt[sn] = bin((inside(src, r) if apart else 0) or fan(src)).count("1")
         return (sn, cnt[sn])
+
+    def play(fs):
+        for f in fs:
+            f()
 
     l_nx = dma("y", [], "lnx", T.nxi[:], T.nx[:])
     l_sy = dma("s", [], "lsy", T.syr[:], T.sy[:])
@@ -110,141 +127,188 @@ def rank_program(g, core, T, topo):
     lo = {"allow_small_or_imprecise_dtypes": True}
     c_p = do("p", [], lambda: g.iota(T.pci[:], [[0, 2]], 0, 1))
     c_ig = do("p", [], lambda: g.iota(T.igf[:], [[1, 8], [0, 16]], 0, 0, **lo))
-    c_pf = do("p", [], lambda: g.iota(T.pf[:], [[0, 1]], 0, 1, **lo))
+    if r > 1:
+        c_ev = do("p", [], lambda: g.iota(T.evr[:], [[0, 8], [1, 8], [-100, 2]], 0, 0, **lo))
     c_row = do("p", [], lambda: g.iota(T.rowf[:], [[1, 128]], 0, 0, **lo))
+    c_pf = do("p", [], lambda: g.iota(T.pf[:], [[0, 1]], 0, 1, **lo))
+    if r > 1:
+        c_ramp = do("p", [], lambda: g.iota(T.ramp[:], [[1, 512]], -256, 0, **lo))
     c_io = do("p", [], lambda: g.iota(T.io4[:], [[-1, 4], [1, 32]], 32 * r, 0, **lo))
     c_one = do("v", [], lambda: vec.memset(T.one[:], 1.0))
     c_zero = do("v", [], lambda: vec.memset(T.zero[:], 0)) if r == 0 else None
     P1, CI, CF, CO = T.pci[:, 0:1], T.ci5, T.cf5, T.cols
     ts([c_p], CI[:, 0:1], P1, 4, None, OP.arith_shift_right)
-    ts([], CI[:, 1:2], P1, 15, None, OP.bitwise_and)
     ts([], CI[:, 2:3], P1, 1, 7, OP.arith_shift_right, OP.bitwise_and)
     ts([], CI[:, 3:4], P1, 1, None, OP.bitwise_and)
+    ts([], CI[:, 1:2], P1, 15, None, OP.bitwise_and)
     x = ts([], CI[:, 4:5], P1, 4, 1, OP.arith_shift_right, OP.bitwise_and)
     c_cf = do("v", [x], lambda: vec.tensor_copy(CF[:], CI[:]))
     c_bo = ts([c_cf, c_ig], T.bo[:], T.igf[:], CF[:, 0:1], None, OP.is_equal)
+    m_sy = ts([l_sy], T.syb[:], T.syr[:], -16.0, None, OP.add)
+    if r > 1:
+        ts([c_ev], T.evh[:], T.evr[:], float(first), 64.0, OP.is_ge, OP.mult)
+        c_evl = ts([], T.evl[:], T.evr[:], float(first), None, OP.is_ge)
+        do("t", [c_bo], lambda: mm(T.pc[:, 0:128], T.bo[:], T.bo[:], True, False))
+        do("t", [c_evl], lambda: mm(T.pc[:, 0:128], T.one[:], T.evh[:], False, False))
+        m_o = do("t", [m_sy], lambda: mm(T.pc[:, 0:128], T.one[:], T.syb[:], False, True))
+    do("t", [c_bo], lambda: mm(T.px[:, 0:128], T.bo[:], T.bo[:], True, False))
+    m_x = do("t", [m_sy, c_one], lambda: mm(T.px[:, 0:128], T.one[:], T.syb[:], False, True))
+    m_ta = ts([l_nx], T.ti[:, 0:128], T.nxi[:, 0:128], 511, None, OP.bitwise_and)
+    m_ti = ts([], T.ti[:, 128:256], T.nxi[:, 128:256], 511, None, OP.bitwise_and)
     x = ts([], CO[:, 2:3], CF[:, 3:4], 100.0, CF[:, 2:3], OP.mult, OP.add)
     c_k0 = ts([], CO[:, 0:1], CF[:, 3:4], -100.0, CF[:, 2:3], OP.mult, OP.add)
-    c_bom = ts([c_bo], T.bom[:], T.bo[:], -4.0, None, OP.mult)
-    c_k1 = ts([x], CO[:, 1:2], CO[:, 2:3], -100.0, None, OP.add)
-    c_mask = ts([c_row], T.mask[:], T.rowf[:, 0:16], CF[:, 1:2], None, OP.is_equal)
     if r > 0:
         ne = do("v", [], lambda: vec.tensor_tensor(CO[:, 4:5], CF[:, 4:5], CF[:, 3:4], OP.not_equal))
         gt = do("v", [], lambda: vec.tensor_tensor(CO[:, 5:6], CF[:, 3:4], CF[:, 4:5], OP.is_gt))
-        c_id = ts([c_pf], T.idn[:], T.rowf[:], T.pf[:], None, OP.is_equal)
-        k = ts([ne], CO[:, 6:7], CO[:, 4:5], 256.0, CF[:, 2:3], OP.mult, OP.add)
         do("v", [], lambda: vec.memset(T.tq[:, 0:16], 0.0))
-        k = ts([k], CO[:, 7:8], CF[:, 4:5], 16.0, CO[:, 6:7], OP.mult, OP.add)
+        k = ts([ne], CO[:, 6:7], CO[:, 4:5], 256.0, CF[:, 2:3], OP.mult, OP.add)
         do("v", [], lambda: vec.memset(T.tq[:, 272:288], 0.0))
-        k = ts([k, gt], CO[:, 8:9], CO[:, 5:6], 32.0, CO[:, 7:8], OP.mult, OP.add)
-        c_k9 = ts([k], CO[:, 9:10], CO[:, 8:9], 8.0, None, OP.add)
-        for m in range(4 if r == 1 else 0, 8):
-            c_im = do("s", [c_id, c_mask], lambda: act(T.idm[:, 128 * m:128 * m + 128], T.idn[:], AF.Copy,
-                                                       scale=T.mask[:, 2 * m + 1:2 * m + 2]))
-    do("t", [c_bom, c_one], lambda: mm(T.px[:, 0:128], T.bo[:], T.bom[:], True, False))
-    m_sy = ts([l_sy], T.syb[:], T.syr[:], 64.0, None, OP.add)
-    m_x = do("t", [m_sy], lambda: mm(T.px[:, 0:128], T.one[:], T.syb[:], False, True))
-    ts([m_x, c_k0], T.sel[:, 0:128], T.px[:, 0:128], CO[:, 0:1], None, OP.is_equal)
-    m_ta = ts([l_nx], T.ti[:, 0:128], T.nxi[:, 0:128], 511, None, OP.bitwise_and)
-    m_ti = ts([], T.ti[:, 128:256], T.nxi[:, 128:256], 511, None, OP.bitwise_and)
-    m_s1 = ts([c_k1], T.sel[:, 128:256], T.px[:, 0:128], CO[:, 1:2], None, OP.is_equal)
+        k = ts([k], CO[:, 7:8], CF[:, 4:5], 16.0, CO[:, 6:7], OP.mult, OP.add)
+    so, po, mo = (T.selo, T.pc, m_o) if r > 1 else (T.sel, T.px, m_x)
     ts([m_ta], T.tb[:, 0:128], T.ti[:, 0:128], -256.0, None, OP.add)
     m_tb = ts([m_ti], T.tb[:, 128:256], T.ti[:, 128:256], -256.0, None, OP.add)
+    c_k1 = ts([x], CO[:, 1:2], CO[:, 2:3], -100.0, None, OP.add)
+    ts([mo, c_k0], so[:, 0:128], po[:, 0:128], CO[:, 0:1], None, OP.is_equal)
+    m_s1 = ts([c_k1], so[:, 128:256], po[:, 0:128], CO[:, 1:2], None, OP.is_equal)
+    if r > 0:
+        k = ts([k, gt], CO[:, 8:9], CO[:, 5:6], 32.0, CO[:, 7:8], OP.mult, OP.add)
+    if r > 1:
+        ts([m_x], T.selc[:, 0:128], T.px[:, 0:128], CO[:, 0:1], CODE, OP.is_equal, OP.mult)
+        m_sf = ts([], T.selc[:, 128:256], T.px[:, 0:128], CO[:, 1:2], CODE, OP.is_equal, OP.mult)
+    c_mask = ts([c_row], T.mask[:], T.rowf[:, 0:16], CF[:, 1:2], None, OP.is_equal)
+    if r > 0:
+        c_k9 = ts([k], CO[:, 9:10], CO[:, 8:9], 8.0, None, OP.add)
+    c_tri = do("p", [c_bo], lambda: g.affine_select(T.tri[:], T.bo[:], [[1, 128]], OP.is_gt, 0.0, 0, -1))
+
+    def late_constants():
+        th = ts([], T.thr[:], T.rowf[:, 0:4], -3.0, CODE, OP.add, OP.mult)
+        return ts([], T.gind[:], T.rowf[:, 0:8], CF[:, 0:1], None, OP.is_equal), th
 
     def window_ab(sel, tb, w, deps):
         a = do("t", deps, lambda: mm(T.pwa[:, 0:256], sel[:, 0:128], tb[:], True, True))
         b = do("t", [], lambda: mm(T.pwb[:, 0:256], sel[:, 128:256], tb[:], True, True))
-        va = do("v", [a], lambda: vec.tensor_copy(w[:, 0:256], T.pwa[:, 0:256]))
-        sb = do("s", [b], lambda: act(w[:, 256:512], T.pwb[:, 0:256], AF.Copy))
-        return [va, sb]
+        sa = do("s", [a], lambda: act(w[:, 0:256], T.pwa[:, 0:256], AF.Copy))
+        vb = do("v", [b], lambda: vec.tensor_copy(w[:, 256:512], T.pwb[:, 0:256]))
+        return [sa, vb]
 
-    def window_mm(sel, tb, deps):
-        do("t", deps, lambda: mm(T.pwa[:, 0:256], sel[:, 0:128], tb[:], True, True))
-        return do("t", [], lambda: mm(T.pwa[:, 256:512], sel[:, 128:256], tb[:], True, True))
+    def window_all(sel, tb, deps, pairs):
+        for h in range(2):
+            c = slice(256 * h, 256 * h + 256)
+            d = do("t", deps, lambda: mm(T.pwa[:, c], sel[:, 128 * h:128 * h + 128], tb[:], True, not pairs))
+            if pairs:
+                d = do("t", [c_ramp, c_evl], lambda: mm(T.pwa[:, c], T.evl[:], T.ramp[:, c], False, True))
+        return d
 
     def window_out(w, d):
         return [do("s", [d], lambda: act(w[:], T.pwa[:], AF.Copy))]
 
-    def code_table():
-        ts([l_em], T.hi[:], T.emi[:], 18, None, OP.arith_shift_right)
-        b = ts([], T.ya[:], T.nxi[:], 2048.0, 64.0, OP.is_lt, OP.mult)
-        ts([], T.ci[:], T.nxi[:], 9, None, OP.arith_shift_right)
-        n = do("v", [b], lambda: vec.tensor_tensor(T.na[:], T.hi[:], T.ya[:], OP.min))
-        z = do("v", [n], lambda: vec.tensor_tensor(T.za[:], T.ci[:], T.na[:], OP.subtract))
-        z = ts([z], T.zb[:], T.za[:], -4.0, 262144.0, OP.add, OP.mult)
-        return do("v", [z], lambda: vec.tensor_tensor(T.ec[:], T.zb[:], T.emi[:], OP.add))
+    def em_float():
+        return ts([l_em], T.emf[:], T.emi[:], -4 * CODE, None, OP.add)
 
-    def code_mm(sf, ec, deps):
-        do("t", deps, lambda: mm(T.pew[:, 0:256], sf[:, 0:128], ec[:], True, True))
-        return do("t", [], lambda: mm(T.pew[:, 256:512], sf[:, 128:256], ec[:], True, True))
+    def code_parts(c0, c1):
+        c = slice(c0, c1)
 
-    def code_out(w, d):
-        return do("s", [d], lambda: act(w[:], T.pew[:], AF.Copy))
+        def a0():
+            ts([l_em], T.hi[:, c], T.emi[:, c], 18, None, OP.arith_shift_right)
 
-    def float_sel(sf, sel, deps):
-        return do("s", deps, lambda: act(sf[:], sel[:], AF.Copy))
+        def a1():
+            ts([l_nx], T.pb[:, c], T.nxi[:, c], 2048.0, 64.0, OP.is_lt, OP.mult)
+
+        def a2():
+            ts([], T.ci[:, c], T.nxi[:, c], 9, None, OP.arith_shift_right)
+        return [a0, a1, a2]
+
+    def code_rest():
+        n = do("v", [("v", cnt["v"])], lambda: vec.tensor_tensor(T.pb[:, 256:512], T.hi[:], T.pb[:, 0:256], OP.min))
+        return do("v", [n], lambda: vec.tensor_tensor(T.za[:], T.ci[:], T.pb[:, 256:512], OP.subtract))
+
+    def code_mm(banks, sf, em, sc, za, dep_em, dep_za):
+        def numbers(h):
+            c = slice(128 * h, 128 * h + 128)
+            return lambda: do("t", dep_em, lambda: mm(banks[h][:, 0:256], sf[:, c], em[:], True, False))
+
+        def counts():
+            for h in range(2):
+                c = slice(128 * h, 128 * h + 128)
+                d = do("t", dep_za, lambda: mm(banks[h][:, 0:256], sc[:, c], za[:], False, True))
+            return d
+        return [numbers(0), numbers(1), counts]
+
+    def code_out(banks, w, d):
+        do("s", [d], lambda: act(w[:, 0:256], banks[0][:, 0:256], AF.Copy))
+        return do("s", [d], lambda: act(w[:, 256:512], banks[1][:, 0:256], AF.Copy))
+
+    def scaled(out, src, by, deps):
+        return do("s", deps, lambda: act(out[:], src[:], AF.Copy, scale=by))
+
+    em_box, id_box = [None], [None, None]
+    each = 1 if r == 1 else 2
 
     def lists():
         sf = do("v", [l_sc], lambda: vec.tensor_copy(CO[:, 3:4], T.syc[:]))
         ti = ts([l_tp], T.tpi[:], T.tp[:], 511, None, OP.bitwise_and)
+        if r > 1:
+            em_box[0] = em_float()
         d = ts([sf, c_mask], T.d16[:], T.mask[:], CO[:, 3:4], None, OP.mult)
         am = do("t", [d], lambda: mm(T.py[:, 64:80], T.bo[:], T.d16[:], True, True))
         tq = do("v", [ti], lambda: vec.tensor_copy(T.tq[:, 16:272], T.tpi[:]))
-        ts([am, c_k9], T.ot[:, 0:16:2], T.py[:, 64:80:2], 32.0, CO[:, 8:9], OP.mult, OP.add)
+        id_box[0] = ts([c_pf], T.idn[:], T.rowf[:], T.pf[:], None, OP.is_equal)
+        id_box[1] = ts([], T.pm[:], T.rowf[:, 0:8], CF[:, 2:3], None, OP.is_equal)
+        n = 32 // each
+        ts([am, c_k9], T.ot[:, 0:n:2], T.py[:, 64:80:each], 32.0, CO[:, 8:9], OP.mult, OP.add)
         do("v", [tq], lambda: vec.transpose(T.tab[:, 0:256], T.tq[:, 16:272]))
-        o = ts([], T.ot[:, 1:16:2], T.py[:, 64:80:2], 32.0, CO[:, 9:10], OP.mult, OP.add)
+        o = ts([], T.ot[:, 1:n:2], T.py[:, 64:80:each], 32.0, CO[:, 9:10], OP.mult, OP.add)
         tr = do("v", [tq], lambda: vec.transpose(T.tab[:, 256:544], T.tq[:, 0:288]))
-        return do("v", [tr, o], lambda: vec.tensor_copy(T.lt[:], T.tab[:].indirect(T.ot[:])))
+        n0, n1 = (2 * FOURS[0], 30) if r == 1 else (2 * first, 16)
+        return do("v", [tr, o], lambda: vec.tensor_copy(T.lt[:, 16 * n0:16 * n1], T.tab[:].indirect(T.ot[:, n0:n1])))
 
-    def own_pair(m):
-        return T.cp[:, 512 * m:512 * m + 512]
+    def joined(n):
+        return T.cp[:, 512 * n:512 * n + 512]
 
-    def join(m, deps, qn):
-        out, src = own_pair(m), T.w[:].indirect(T.lt[:, 32 * m:32 * m + 32])
+    def join(n, win, j, deps, qn, m):
+        i = 32 * (j // each)
+        out, src = joined(n), win.indirect(T.lt[:, i:i + 32])
+        keep = 1.0 if m is None else T.pm[:, m:m + 1]
         if qn == "v":
-            return do("v", deps, lambda: vec.tensor_copy(out, src))
-        return do("s", deps, lambda: act(out, src, AF.Copy))
-
-    def merge(cpd, order):
-        for n, m in enumerate(order):
-            d = do("t", [cpd[m], c_im], lambda: mm(T.pcm[:], T.idm[:, 128 * m:128 * m + 128], own_pair(m),
-                                                   n == 0, n == len(order) - 1))
-        return do("s", [d], lambda: act(T.cpm[:], T.pcm[:], AF.Copy))
+            return ts(deps + id_box, out, src, keep, None, OP.mult)
+        return do("s", deps + id_box, lambda: act(out, src, AF.Copy, scale=keep))
 
     def gather(win, at, deps, k, col):
         b = col - k
         tile, x0, d = at
         return (T.tt, col, ts([d] + deps, T.tt[:, b:b + 16], win.indirect(tile[:, x0:x0 + 1]), 256.0, None, OP.add))
 
-    def plain(at, w, deps, j, reg):
-        return gather(w[:], at, deps, (j - 1) % 16, reg + 16 + 18 * j)
+    def code_at(qn, reads, j, ewin, edep, ee):
+        tile, x0, d = reads[j]
+        b = 0 if j == 0 else 16 * j + 16
+        out, src = ee[:, b:b + 16], ewin[:].indirect(tile[:, x0:x0 + 1])
+        if qn == "v":
+            return ts([d, edep, c_mask], out, src, T.mask[:, j:j + 1], None, OP.mult)
+        return do("s", [d, edep, c_mask], lambda: act(out, src, AF.Copy, scale=T.mask[:, j:j + 1]))
 
-    def follow(reads, ewin, edep, ee, first=0, end=16):
-        last = None
-        for j in range(first, end):
-            tile, x0, d = reads[j]
-            b = 0 if j == 0 else 16 * j + 16
-            last = do("s", [d, edep, c_mask], lambda: act(
-                ee[:, b:b + 16], ewin[:].indirect(tile[:, x0:x0 + 1]), AF.Copy, scale=T.mask[:, j:j + 1]))
+    def follow(reads, ewin, edep, ee, steps):
+        for j in steps:
+            last = code_at("s", reads, j, ewin, edep, ee)
         return last
 
-    def paired(at, pw, w, deps, reg, last_too, fill):
+    def string(q, at, w, wdep, pw, pdep, reg, hooks, last_too):
         reads = []
-        for m in range(8):
-            k = (2 * m - 1) % 16
-            nxt = None
-            if m < 7 or last_too:
-                nxt = gather(pw(m), at, deps, k, reg + 16 + 18 * m)
-            reads += [at, gather(w[:], at, deps, k, reg + 196 + 18 * m)]
-            at = nxt
-            if m > 1 and fill:
-                fill.pop(0)()
+        for j in range(16):
+            reads.append(at)
+            pair = j >= 2 * FIRST.get(q, 8)
+            if not (pair and j % 2):
+                k, col = (j - 1) % 16, reg + 16 + 18 * j
+                if pair:
+                    at = gather(pw(j // 2), at, pdep(j // 2), k, col)
+                elif j < 15 or last_too:
+                    at = gather(w[:], at, wdep, k, col)
+            play(hooks.get(j, []))
         return reads, at
 
     gd, ed_, ydep = {}, {}, [None, 0]
 
     def total(ee, last, out):
-        return do("v", [last], lambda: vec.tensor_reduce(out[:], ee[:, 15:271:17], AxisListType.X, OP.add))
+        return do("v", last, lambda: vec.tensor_reduce(out[:], ee[:, 15:271:17], AxisListType.X, OP.add))
 
     def gates(q, code, dep):
         gd[q] = ts([dep, c_thr], T["g4%d" % q][:], T.thr[:], code[:], None, OP.is_le)
@@ -271,53 +335,58 @@ def rank_program(g, core, T, topo):
     def decode(q, code, dep):
         return [lambda: gates(q, code, dep)] + digits(q, code, dep)
 
-    def play(fs):
-        for f in fs:
-            f()
-
-    banks = {0: T.pb, 1: T.pc, 2: T.px, 3: T.pb}
+    banks = {0: T.pb, 1: T.pc, 2: T.pcm, 3: T.pb}
+    free = {}
     begun = {}
     bdep = {}
 
     def count(q, b, stop=False):
-        bank = banks[q]
-        for m in range(4):
-            bdep[q] = do("t", [gd[b], c_tri], lambda: mm(bank[:, 0:1], (T.tri if b == q else T.bo)[:], T["g4%d" % b][:, m:m + 1],
-                                                         q not in begun, stop and m == 3))
+        n = 1 if q == 3 else 4
+        for m in range(0, 4, n):
+            bdep[q] = do("t", [gd[b], c_tri, free.get(q)], lambda: mm(
+                banks[q][:, 0:n], (T.tri if b == q else T.bo)[:], T["g4%d" % b][:, m:m + n], q not in begun, stop and m + n == 4))
             begun[q] = True
 
+    def position(q):
+        if q < 3:
+            bdep[q] = do("v", [bdep[q]], lambda: vec.tensor_reduce(T.pos[:, q:q + 1], banks[q][:, 0:4], AxisListType.X, OP.add))
+
     def place(q, final):
-        bank, oh, ep = banks[q], T["oh%d" % q], T["ep%d" % q]
+        oh, ep = T["oh%d" % q], T["ep%d" % q]
 
         def one(m):
-            o = ts([bdep[q], ed_[q], c_io], oh[:, 32 * m:32 * m + 32], T.io4[:, 32 * m:32 * m + 32], bank[:, 0:1],
-                   ep[:, m:m + 1], OP.is_equal, OP.mult)
+            o = ts([bdep[q], ed_[q], c_io], oh[:, 32 * m:32 * m + 32], T.io4[:, 32 * m:32 * m + 32],
+                   T.pos[:, q:q + 1] if q < 3 else banks[q][:, 0:1], ep[:, m:m + 1], OP.is_equal, OP.mult)
             ydep[0] = do("t", [o, c_gi], lambda: mm(
                 T.py[0:8, 0:32], T.gind[:], oh[:, 32 * m:32 * m + 32], ydep[1] == 0, final and m == 3))
             ydep[1] += 1
-        return [lambda: one(0), lambda: one(1), lambda: one(2), lambda: one(3)]
-
-    def late_constants():
-        a = ts([c_row, c_pf], T.tri0[:], T.rowf[:], T.pf[:], None, OP.is_gt)
-        th = ts([], T.thr[:], T.rowf[:, 0:4], -3.0, 262144.0, OP.add, OP.mult)
-        gi = ts([], T.gind[:], T.rowf[:, 0:8], CF[:, 0:1], None, OP.is_equal)
-        return do("v", [a], lambda: vec.tensor_tensor(T.tri[:], T.tri0[:], T.bo[:], OP.mult)), gi, th
+        return [lambda: position(q), lambda: one(0), lambda: one(1), lambda: one(2), lambda: one(3)]
 
     if r == 0:
         wdep = window_ab(T.sel, T.tb, T.w, [m_s1, m_tb])
-        at = (T.zero, 0, c_zero)
-        reads = []
-        for j in range(16):
-            reads.append(at)
-            at = plain(at, T.w, wdep, j, 0)
+        sfd = scaled(T.self, T.sel, 1.0, [m_s1])
+        scd = scaled(T.selc, T.sel, CODE, [m_s1])
+        parts = []
+        for c in range(0, 256, 64):
+            parts += code_parts(c, c + 64)
+        hooks = {}
+        for n in range(len(parts)):
+            hooks[n + 2] = [parts[n]]
+        reads, at = string(0, (T.zero, 0, c_zero), T.w, wdep, None, None, 0, hooks, True)
         s1 = T.tt[:, at[1]:at[1] + 2]
         send([at[2]], [2, 3], "s1", s1, "as1")
         send([], [1], "s1", s1, "as1")
-        sfd = float_sel(T.self, T.sel, [m_s1])
-        ecd = code_table()
-        c_tri, c_gi, c_thr = late_constants()
-        ed = code_out(T.e, code_mm(T.self, T.ec, [sfd, ecd]))
-        oc = total(T.eea, follow(reads, T.e, ed, T.eea), T.oca)
+        emd = em_float()
+        zad = code_rest()
+        cb = (T.pew, T.pcm)
+        fs = code_mm(cb, T.self, T.emf, T.selc, T.za, [sfd, emd], [scd, zad])
+        play(fs[:2])
+        ed = code_out(cb, T.e, fs[2]())
+        c_gi, c_thr = late_constants()
+        last = follow(reads, T.e, ed, T.eea, range(0, 16, 2))
+        for j in range(1, 16, 2):
+            last_v = code_at("v", reads, j, T.e, ed, T.eea)
+        oc = total(T.eea, [last, last_v], T.oca)
         send([oc], [2, 3, 1], "rc0", T.oca[:], "arc0")
         play(decode(0, T.oca, oc))
         count(0, 0, True)
@@ -329,140 +398,164 @@ def rank_program(g, core, T, topo):
         play(digits(1, T.rc1, a1))
         play(place(1, True))
     elif r == 1:
-        wdep = window_ab(T.sel, T.tb, T.w, [m_s1, m_tb])
-        send(wdep, [2, 3], "w1", T.w[:], "aw1")
-        sfd = float_sel(T.self, T.sel, [m_s1])
+        wdep = window_out(T.w, window_all(T.sel, T.tb, [m_s1, m_tb], False))
+        send(wdep, [2, 3], "w1", T.w[:], "aw1", True)
         ltd = lists()
-        cpd = {}
-        for m in (4, 5, 6, 7):
-            cpd[m] = join(m, wdep + [ltd], "v" if m % 2 else "s")
-        cmd = merge(cpd, [4, 5, 6, 7])
-        send([cmd], [2, 3], "cp1", T.cpm[:], "acp1")
-        for m in (0, 1):
-            cpd[m] = join(m, wdep + [ltd], "s")
-        ecd = code_table()
-        for m in (2, 3):
-            cpd[m] = join(m, wdep + [ltd], "v")
-        c_tri, c_gi, c_thr = late_constants()
-        ed = code_out(T.e, code_mm(T.self, T.ec, [sfd, ecd]))
-        axs = arrive(3, "aselx")
-        sfx = float_sel(T.selfx, T.selx, [axs])
-        wxm = window_mm(T.selx, T.tbx, wdep + [axs, arrive(3, "atbx")])
-        exm = code_mm(T.selfx, T.ecx, [sfx, arrive(3, "aecx"), ed])
-        at = (T.s1, 0, arrive(0, "as1"))
-        reads, at = paired(at, own_pair, T.w, wdep + list(cpd.values()), 0, True, [])
-        last = follow(reads, T.e, ed, T.eea, 0, 8)
-        wxd = window_out(T.wx, wxm)
-        last = follow(reads, T.e, ed, T.eea, 8, 16)
-        exd = code_out(T.ex, exm)
-        reads = []
-        fill = []
-        for j in range(16):
-            reads.append(at)
-            if j < 15:
-                at = plain(at, T.wx, wxd, j, 360)
-            if j == 1:
-                oc = total(T.eea, last, T.oca)
-                send([oc], [2, 3, 0], "rc1", T.oca[:], "arc1")
-                fill = decode(1, T.oca, oc) + decode(0, T.rc0, arrive(0, "arc0"))
-            elif fill:
-                fill.pop(0)()
-        last = follow(reads, T.ex, exd, T.eeb)
-        play(fill)
+        va, sa = FOURS
+        dv = join(0, T.w[:], va + 2, wdep + [ltd], "v", None)
+        ds = join(3, T.w[:], sa + 2, wdep + [ltd], "s", None)
+        emd = em_float()
+        dv = join(1, joined(0), va + 1, [dv], "v", None)
+        ds = join(4, joined(3), sa + 1, [ds], "s", None)
+        parts = code_parts(0, 256)
+        parts[0]()
+        dv = join(2, joined(1), va, [dv], "v", (va + 3) // 2)
+        ds = join(5, joined(4), sa, [ds], "s", (sa + 3) // 2)
+        play(parts[1:])
+        md = []
+        for n, d in ((2, dv), (5, ds)):
+            for h in range(2):
+                x = 512 * n + 256 * h
+                md.append(do("t", [d] + id_box, lambda: mm((T.pcm, T.px)[h][:, 0:256], T.idn[:], T.cp[:, x:x + 256],
+                                                           n == 2, n == 5)))
+        cmd = [do("v", [md[2]], lambda: vec.tensor_copy(T.cpm[:, 0:256], T.pcm[:, 0:256])),
+               do("s", [md[3]], lambda: act(T.cpm[:, 256:512], T.px[:, 0:256], AF.Copy))]
+        free[2] = cmd[0]
+        send(cmd, [2, 3], "cp1", T.cpm[:], "acp1", True)
+        sfd = scaled(T.self, T.sel, 1.0, [m_s1])
+        scd = scaled(T.selc, T.sel, CODE, [m_s1])
+        zad = code_rest()
+        cb = (T.pew, T.pwb)
+        fs = code_mm(cb, T.self, T.emf, T.selc, T.za, [sfd, emd], [scd, zad])
+        play(fs[:2])
+        ed = code_out(cb, T.e, fs[2]())
+        reads = string(1, (T.s1, 0, arrive(0, "as1")), T.w, wdep, None, None, 0, {}, False)[0]
+        last = follow(reads, T.e, ed, T.eea, range(15))
+        c_gi, c_thr = late_constants()
+        last_v = code_at("v", reads, 15, T.e, ed, T.eea)
+        oc = total(T.eea, [last, last_v], T.oca)
+        send([oc], [2, 3, 0], "rc1", T.oca[:], "arc1", True)
+        play(decode(1, T.oca, oc))
+        count(1, 1)
+        a0 = arrive(0, "arc0")
+        gates(0, T.rc0, a0)
+        count(1, 0, True)
         count(0, 0, True)
-        count(1, 0)
-        count(1, 1, True)
         count(2, 0)
         count(2, 1)
+        play(digits(0, T.rc0, a0))
         play(place(0, False))
         play(place(1, False))
-        oc = total(T.eeb, last, T.ocb)
-        gates(2, T.ocb, oc)
+        a2 = arrive(3, "arc2")
+        gates(2, T.rc2, a2)
         count(2, 2, True)
-        play(digits(2, T.ocb, oc))
+        play(digits(2, T.rc2, a2))
         play(place(2, True))
     else:
         o = 5 - r
-        wdep = window_out(T.w, window_mm(T.sel, T.tb, [m_s1, m_tb]))
-        sfd = float_sel(T.self, T.sel, [m_s1])
-        send([m_s1], [o], "selx", T.sel[:], "aselx")
-        send([m_tb], [o], "tbx", T.tb[:], "atbx")
+        wdep = window_out(T.w, window_all(T.selo, T.tb, [m_s1, m_tb], True))
+        sfd = scaled(T.self, T.selc, 1.0 / CODE, [m_sf])
+        send([m_sf], [o], "selx", T.selc[:], "aselx")
         ltd = lists()
-        cpd = {}
-        for m in (0, 1, 2, 4, 5, 6):
-            cpd[m] = join(m, wdep + [ltd], "s")
-        ecd = code_table()
-        send([ecd], [o], "ecx", T.ec[:], "aecx")
-        for m in (3, 7):
-            cpd[m] = join(m, wdep + [ltd], "v")
-        cmd = merge(cpd, [0, 1, 2, 3, 4, 5, 7, 6])
-        axs, axt, axe = arrive(o, "aselx"), arrive(o, "atbx"), arrive(o, "aecx")
-        if r == 3:
-            send([axs], [1], "selx", T.selx[:], "aselx")
-            send([axt], [1], "tbx", T.tbx[:], "atbx")
-            send([axe], [1], "ecx", T.ecx[:], "aecx")
+        emd = em_box[0]
+        send([emd], [o], "emx", T.emf[:], "aemx")
+        if first:
+            send(wdep, [o], "wx", T.w[:], "awx")
+        on_s, made = list(range(first, 5)), {}
+        axs = arrive(o, "aselx")
+        between = 2 if r == 3 else len(on_s)
+        for m in on_s[:between]:
+            made[m] = join(m, T.w[:], 2 * m, wdep + [ltd], "s", m)
+        sfx = scaled(T.selfx, T.selx, 1.0 / CODE, [axs])
+        for m in on_s[between:]:
+            made[m] = join(m, T.w[:], 2 * m, wdep + [ltd], "s", m)
+        for m in (5, 6, 7):
+            made[m] = join(m, T.w[:], 2 * m, wdep + [ltd], "v", m)
+        play(code_parts(0, 256))
+        zad = code_rest()
+        send([zad], [o], "zax", T.za[:], "azax")
+        own_banks, other_banks = (T.pew, T.pwb), (T.px, T.pwa)
+        axe, axz = arrive(o, "aemx"), arrive(o, "azax")
+        own = code_mm(own_banks, T.self, T.emf, T.selc, T.za, [sfd, emd], [zad])
+        other = code_mm(other_banks, T.selfx, T.emx, T.selx, T.zax, [sfx, axe, m_sf, wdep[0]], [axz])
+        codes = {r: (own, own_banks, T.e), o: (other, other_banks, T.ex)}
+        code2, code3 = codes[2][0], codes[3][0]
+        e2, e3 = codes[2][2], codes[3][2]
+        order = [5, on_s[0], 6, on_s[1], 7] + on_s[2:]
+        for n in range(len(order)):
+            if r == 3 and n == 5:
+                code2.pop(0)()
+            m = order[n]
+            md = do("t", [made[m]] + id_box, lambda: mm(T.pcm[:], T.idn[:], joined(m), n == 0, n == len(order) - 1))
+        cmd = do("s", [md], lambda: act(T.cpm[:], T.pcm[:], AF.Copy))
+        free[2] = cmd
         send([cmd], [o], "cpx", T.cpm[:], "acpx")
-        c_tri, c_gi, c_thr = late_constants()
-        sfx = float_sel(T.selfx, T.selx, [axs])
-        wxd = window_out(T.wx, window_mm(T.selx, T.tbx, wdep + [axs, axt]))
-        codes = {r: (T.self, T.ec, [sfd, ecd], T.e), o: (T.selfx, T.ecx, [sfx, axe], T.ex)}
-        e2, e3 = codes[2][3], codes[3][3]
-        e2d = code_out(e2, code_mm(codes[2][0], codes[2][1], codes[2][2]))
-        m3 = code_mm(codes[3][0], codes[3][1], codes[3][2] + [e2d])
-
+        play(code2[:-1])
+        e2d = code_out(codes[2][1], e2, code2[-1]())
+        play(code3[:-1])
+        m3 = code3[-1]()
+        aw1, acp1 = [arrive(1, "aw1", True)], [arrive(1, "acp1", True)]
+        awx, acpx = [arrive(o, "awx")] if FIRST[o] else [], [arrive(o, "acpx")]
         at = (T.s1, 0, arrive(0, "as1"))
-        aw1, acp1 = [arrive(1, "aw1")], [arrive(1, "acp1")]
-        for j in range(8):
-            at = plain(at, T.w1, aw1, j, 0)
-        for m in range(4, 8):
-            at = gather(T.cp1[:], at, acp1, 2 * m - 1, 16 + 36 * m)
-        runs = {r: (own_pair, T.w, wdep + list(cpd.values())),
-                o: (lambda m: T.cpx[:], T.wx, wxd + [arrive(o, "acpx")])}
-        pw, w, deps = runs[2]
-        reads, at = paired(at, pw, w, deps, 320, True, [])
-        last = follow(reads, e2, e2d, T.eea)
-        e3d = code_out(e3, m3)
+        for j in range(FOURS[0]):
+            at = gather(T.w1[:], at, aw1, (j - 1) % 16, 16 + 18 * j)
+            if j == 0:
+                c_gi, c_thr = late_constants()
+        for j in FOURS:
+            at = gather(T.cp1[:], at, acp1, j - 1, 16 + 18 * j)
+        runs = {r: (T.w, wdep, joined, lambda m: [made[m]]), o: (T.wx, awx, lambda m: T.cpx[:], lambda m: acpx)}
+        reads, at = string(2, at, *runs[2], 320, {}, True)
+        last = follow(reads, e2, e2d, T.eea, range(16))
+        e3d = code_out(codes[3][1], e3, m3)
+        a0, a1 = arrive(0, "arc0"), arrive(1, "arc1", True)
         box = {}
-        a0, a1 = arrive(0, "arc0"), arrive(1, "arc1")
+
+        def g0():
+            gates(0, T.rc0, a0)
+            for q in range(1 if r == 2 else 2, 4):
+                count(q, 0)
 
         def t2():
-            box[0] = total(T.eea, last, T.oca)
+            box[2] = total(T.eea, [last], T.oca)
+            if r == 3:
+                send([box[2]], [1], "rc2", T.oca[:], "arc2")
 
-        def t3():
-            box[1] = total(T.eeb, last3, T.ocb)
-        fill = [lambda: gates(0, T.rc0, a0), t2, lambda: gates(2, T.oca, box[0])] + digits(2, T.oca, None)
-        pw, w, deps = runs[3]
-        reads, _x = paired(at, pw, w, deps, 680, False, fill)
-        last3 = follow(reads, e3, e3d, T.eeb)
-        if r == 2:
-            count(1, 0)
-        count(2, 0)
-        count(2, 2)
-        count(3, 0)
-        count(3, 2)
-        gates(1, T.rc1, a1)
-        if r == 2:
-            count(1, 1, True)
-            fill += digits(1, T.rc1, a1)
-        count(2, 1, True)
-        count(3, 1)
-        todo = [t3, lambda: gates(3, T.ocb, box[1])] + digits(3, T.ocb, None)
-        if r == 2:
-            fill += place(1, False)
-        fill += place(2, False)
-        for n in range(len(todo)):
-            play(todo[n:n + 1] + fill[n:n + 1])
-            if n == 1:
-                count(3, 3, True)
-        play(fill[len(todo):])
+        def g2():
+            gates(2, T.oca, box[2])
+            count(2, 2)
+            count(3, 2)
+
+        def g1():
+            gates(1, T.rc1, a1)
+            if r == 2:
+                count(1, 1, True)
+            count(2, 1, True)
+            count(3, 1)
+        D2, p2 = digits(2, T.oca, None), place(2, False)
+        D1, p1 = (digits(1, T.rc1, a1), place(1, False)) if r == 2 else ([], [])
+        hooks = {0: [g0], 2: [t2], 4: [g2] + D2[:1], 6: D2[1:2], 8: D2[2:3], 10: D2[3:], 12: [g1] + D1[:1], 14: D1[1:3]}
+        reads3 = string(3, at, *runs[3], 640, hooks, False)[0]
+        last3 = follow(reads3, e3, e3d, T.eeb, range(15))
+        last_v = code_at("v", reads3, 15, e3, e3d, T.eeb)
+        play(D1[3:])
+        oc = total(T.eeb, [last3, last_v], T.ocb)
+        play(p2[:1] + p1[:1])
+        D3 = digits(3, T.ocb, oc)
+        D3[0]()
+        gates(3, T.ocb, oc)
+        count(3, 3, True)
+        play(p2[1:4])
+        play(D3[1:3])
+        play(p2[4:] + p1[1:3])
+        D3[3]()
+        play(p1[3:])
         if r == 3:
-            for b in range(4):
-                for m in range(4):
-                    zd = do("t", [gd[b], e3d], lambda: mm(T.pew[0:8, 0:1], T.gind[:], T["g4%d" % b][:, m:m + 1],
-                                                          b == 0 and m == 0, b == 3 and m == 3))
+            for b in (0, 2, 1, 3):
+                zd = do("t", [gd[b], e3d], lambda: mm(T.pew[0:8, 0:4], T.gind[:], T["g4%d" % b][:], b == 0, b == 3))
         play(place(3, True))
         if r == 3:
-            nd = ts([zd, c_io], T.neg[:], T.io4[0:8, 0:32], T.pew[0:8, 0:1], -1.0, OP.is_ge, OP.mult)
+            zr = do("v", [zd], lambda: vec.tensor_reduce(T.zed[:], T.pew[0:8, 0:4], AxisListType.X, OP.add))
+            nd = ts([zr, c_io], T.neg[:], T.io4[0:8, 0:32], T.zed[:], -1.0, OP.is_ge, OP.mult)
     if r == 3:
         yd = do("v", [ydep[0], nd], lambda: vec.tensor_tensor(T.ysb[:], T.py[0:8, 0:32], T.neg[:], OP.add))
     else:

import numpy as np
from concourse.bass import DstId, RemoteDMATransfer
from concourse.mybir import dt, AluOpType, AxisListType, ActivationFunctionType

F, H, I, U = "float32", "bfloat16", "int32", "uint16"
SCRATCH = {
    "nxi": ("sbuf", [128, 256], I), "emi": ("sbuf", [128, 256], I), "syr": ("sbuf", [1, 128], I),
    "syb": ("sbuf", [1, 128], H), "one": ("sbuf", [1, 128], H), "syc": ("sbuf", [128, 1], I),
    "evr": ("sbuf", [1, 128], F), "evh": ("sbuf", [1, 128], H), "evl": ("sbuf", [1, 128], H), "ramp": ("sbuf", [1, 512], H),
    "pci": ("sbuf", [128, 2], I), "pf": ("sbuf", [128, 1], F), "igf": ("sbuf", [128, 128], F),
    "rowf": ("sbuf", [128, 128], F), "io4": ("sbuf", [128, 128], F),
    "ci5": ("sbuf", [128, 5], I), "cf5": ("sbuf", [128, 5], F), "cols": ("sbuf", [128, 12], F),
    "bo": ("sbuf", [128, 128], H), "tri": ("sbuf", [128, 128], H), "idn": ("sbuf", [128, 128], H),
    "mask": ("sbuf", [128, 16], F), "pm": ("sbuf", [128, 8], F), "gind": ("sbuf", [128, 8], H), "thr": ("sbuf", [128, 4], F),
    "ti": ("sbuf", [128, 256], I), "sel": ("sbuf", [128, 256], H), "selo": ("sbuf", [128, 256], H), "tb": ("sbuf", [128, 256], H),
    "hi": ("sbuf", [128, 256], I), "ci": ("sbuf", [128, 256], I), "za": ("sbuf", [128, 256], H), "emf": ("sbuf", [128, 256], F),
    "self": ("sbuf", [128, 256], F), "selc": ("sbuf", [128, 256], H), "selfx": ("sbuf", [128, 256], F),
    "selx": ("sbuf", [128, 256], H), "emx": ("sbuf", [128, 256], F), "zax": ("sbuf", [128, 256], H),
    "tp": ("sbuf", [128, 256], I), "tpi": ("sbuf", [128, 256], I), "tq": ("sbuf", [128, 288], F), "tab": ("sbuf", [128, 544], F),
    "d16": ("sbuf", [128, 16], H), "ot": ("sbuf", [128, 32], U), "lt": ("sbuf", [128, 512], U),
    "w": ("sbuf", [128, 512], H), "w1": ("sbuf", [128, 512], H), "wx": ("sbuf", [128, 512], H),
    "e": ("sbuf", [128, 512], F), "ex": ("sbuf", [128, 512], F),
    "cp": ("sbuf", [128, 4096], H), "cpm": ("sbuf", [128, 512], H), "cpx": ("sbuf", [128, 512], H), "cp1": ("sbuf", [128, 512], H),
    "s1": ("sbuf", [128, 2], U), "zero": ("sbuf", [128, 2], U), "tt": ("sbuf", [128, 1080], U),
    "eea": ("sbuf", [128, 272], F), "eeb": ("sbuf", [128, 272], F), "pos": ("sbuf", [128, 4], F), "zed": ("sbuf", [8, 1], F),
    "rc0": ("sbuf", [128, 1], F), "rc1": ("sbuf", [128, 1], F), "rc2": ("sbuf", [128, 1], F),
    "oca": ("sbuf", [128, 1], F), "ocb": ("sbuf", [128, 1], F), "ysb": ("sbuf", [8, 32], F), "neg": ("sbuf", [8, 32], F),
    "px": ("psum", [128, 512], F), "pwa": ("psum", [128, 512], F), "pwb": ("psum", [128, 512], F),
    "pcm": ("psum", [128, 512], F), "pew": ("psum", [128, 512], F), "pb": ("psum", [128, 512], F),
    "pc": ("psum", [128, 512], F), "py": ("psum", [128, 512], F),
}
for _q in range(4):
    SCRATCH["qi%d" % _q] = ("sbuf", [128, 1], I)
    SCRATCH["di%d" % _q] = ("sbuf", [128, 4], I)
    SCRATCH["g4%d" % _q] = ("sbuf", [128, 4], H)
    SCRATCH["ep%d" % _q] = ("sbuf", [128, 4], F)
    SCRATCH["oh%d" % _q] = ("sbuf", [128, 128], H)
SEMAPHORES = ["v", "s", "t", "p", "lnx", "lsy", "lsc", "ltp", "lem", "st", "loc",
              "as1", "aw1", "acp1", "awx", "aselx", "aemx", "azax", "acpx", "arc0", "arc1", "arc2"]
OP = AluOpType
AF = ActivationFunctionType
FIRST = {2: 1, 3: 0}
FOURS = (8, 12)
CODE = 262144.0


def rank_program(g, core, T, topo):
    r = T.rank_of(core)
    if r is None:
        return
    Q = {"v": g.vector, "s": g.scalar, "t": g.tensor, "p": g, "y": g.sync}
    cnt = {}
    seen = {}
    vec, act, mm = g.vector, g.scalar.activation, g.tensor.matmul
    first = FIRST.get(r, 8)

    def waits(qn, deps):
        need = {}
        for d in deps:
            if d is not None:
                need[d[0]] = max(need.get(d[0], 0), d[1])
        for sn in need:
            if seen.get((qn, sn), 0) < need[sn]:
                Q[qn].wait_ge(T.sem[sn], need[sn])
                seen[(qn, sn)] = need[sn]

    def do(qn, deps, fn):
        waits(qn, deps)
        fn().then_inc(T.sem[qn], 1)
        cnt[qn] = cnt.get(qn, 0) + 1
        return (qn, cnt[qn])

    def ts(deps, *a):
        return do("v", deps, lambda: vec.tensor_scalar(*a))

    def dma(qn, deps, sn, out, in_):
        waits(qn, deps)
        Q[qn].dma_start(out, in_).then_inc(T.sem[sn], 16)
        cnt[sn] = cnt.get(sn, 0) + 16
        return (sn, cnt[sn])

    def fan(src):
        m = -1
        for c in T.cores:
            if c != T.cores[src]:
                m &= topo.mask(T.cores[src], c)
        return m

    def inside(src, dst):
        if topo.chip(T.cores[src]) != topo.chip(T.cores[dst]):
            return 0
        return topo.mask(T.cores[src], T.cores[dst]) & ~fan(src)

    def send(deps, dsts, name_out, src, sn, apart=False):
        waits("p", deps)
        lanes = {}
        for d in dsts:
            m = (inside(r, d) if apart else 0) or fan(r)
            lanes[m] = lanes.get(m, []) + [d]
        trs = []
        for m in lanes:
            ids = []
            for d in lanes[m]:
                rid, pid, _ = topo.addr(T.cores[d])
                ids.append(DstId(rid=rid, pnc=pid))
            trs.append(RemoteDMATransfer(dst_ids=ids, dma_engine_mask=m, remote_sem=T.sem[sn], srcs=[src],
                                         dsts=[T[name_out][:] for _ in ids], alu_op=0))
            cnt["loc"] = cnt.get("loc", 0) + bin(m).count("1")
        g.remote_dma_fused(trs, local_sem=T.sem.loc)

    def arrive(src, sn, apart=False):
        cnt[sn] = bin((inside(src, r) if apart else 0) or fan(src)).count("1")
        return (sn, cnt[sn])

    def play(fs):
        for f in fs:
            f()

    l_nx = dma("y", [], "lnx", T.nxi[:], T.nx[:])
    l_sy = dma("s", [], "lsy", T.syr[:], T.sy[:])
    if r > 0:
        l_sc = dma("s", [], "lsc", T.syc[:], T.sy[:])
        for a in range(8):
            l_tp = dma("y" if a % 2 else "s", [], "ltp", T.tp[:, 32 * a:32 * a + 32], T.nx[:, 512 * a:512 * a + 512])
    l_em = dma("y", [], "lem", T.emi[:], T.em[:])

    lo = {"allow_small_or_imprecise_dtypes": True}
    c_p = do("p", [], lambda: g.iota(T.pci[:], [[0, 2]], 0, 1))
    c_ig = do("p", [], lambda: g.iota(T.igf[:], [[1, 8], [0, 16]], 0, 0, **lo))
    if r > 1:
        c_ev = do("p", [], lambda: g.iota(T.evr[:], [[0, 8], [1, 8], [-100, 2]], 0, 0, **lo))
    c_row = do("p", [], lambda: g.iota(T.rowf[:], [[1, 128]], 0, 0, **lo))
    c_pf = do("p", [], lambda: g.iota(T.pf[:], [[0, 1]], 0, 1, **lo))
    if r > 1:
        c_ramp = do("p", [], lambda: g.iota(T.ramp[:], [[1, 512]], -256, 0, **lo))
    c_io = do("p", [], lambda: g.iota(T.io4[:], [[-1, 4], [1, 32]], 32 * r, 0, **lo))
    c_one = do("v", [], lambda: vec.memset(T.one[:], 1.0))
    c_zero = do("v", [], lambda: vec.memset(T.zero[:], 0)) if r == 0 else None
    P1, CI, CF, CO = T.pci[:, 0:1], T.ci5, T.cf5, T.cols
    ts([c_p], CI[:, 0:1], P1, 4, None, OP.arith_shift_right)
    ts([], CI[:, 2:3], P1, 1, 7, OP.arith_shift_right, OP.bitwise_and)
    ts([], CI[:, 3:4], P1, 1, None, OP.bitwise_and)
    ts([], CI[:, 1:2], P1, 15, None, OP.bitwise_and)
    x = ts([], CI[:, 4:5], P1, 4, 1, OP.arith_shift_right, OP.bitwise_and)
    c_cf = do("v", [x], lambda: vec.tensor_copy(CF[:], CI[:]))
    c_bo = ts([c_cf, c_ig], T.bo[:], T.igf[:], CF[:, 0:1], None, OP.is_equal)
    m_sy = ts([l_sy], T.syb[:], T.syr[:], -16.0, None, OP.add)
    if r > 1:
        ts([c_ev], T.evh[:], T.evr[:], float(first), 64.0, OP.is_ge, OP.mult)
        c_evl = ts([], T.evl[:], T.evr[:], float(first), None, OP.is_ge)
        do("t", [c_bo], lambda: mm(T.pc[:, 0:128], T.bo[:], T.bo[:], True, False))
        do("t", [c_evl], lambda: mm(T.pc[:, 0:128], T.one[:], T.evh[:], False, False))
        m_o = do("t", [m_sy], lambda: mm(T.pc[:, 0:128], T.one[:], T.syb[:], False, True))
    do("t", [c_bo], lambda: mm(T.px[:, 0:128], T.bo[:], T.bo[:], True, False))
    m_x = do("t", [m_sy, c_one], lambda: mm(T.px[:, 0:128], T.one[:], T.syb[:], False, True))
    m_ta = ts([l_nx], T.ti[:, 0:128], T.nxi[:, 0:128], 511, None, OP.bitwise_and)
    m_ti = ts([], T.ti[:, 128:256], T.nxi[:, 128:256], 511, None, OP.bitwise_and)
    x = ts([], CO[:, 2:3], CF[:, 3:4], 100.0, CF[:, 2:3], OP.mult, OP.add)
    c_k0 = ts([], CO[:, 0:1], CF[:, 3:4], -100.0, CF[:, 2:3], OP.mult, OP.add)
    if r > 0:
        ne = do("v", [], lambda: vec.tensor_tensor(CO[:, 4:5], CF[:, 4:5], CF[:, 3:4], OP.not_equal))
        gt = do("v", [], lambda: vec.tensor_tensor(CO[:, 5:6], CF[:, 3:4], CF[:, 4:5], OP.is_gt))
        do("v", [], lambda: vec.memset(T.tq[:, 0:16], 0.0))
        k = ts([ne], CO[:, 6:7], CO[:, 4:5], 256.0, CF[:, 2:3], OP.mult, OP.add)
        do("v", [], lambda: vec.memset(T.tq[:, 272:288], 0.0))
        k = ts([k], CO[:, 7:8], CF[:, 4:5], 16.0, CO[:, 6:7], OP.mult, OP.add)
    so, po, mo = (T.selo, T.pc, m_o) if r > 1 else (T.sel, T.px, m_x)
    ts([m_ta], T.tb[:, 0:128], T.ti[:, 0:128], -256.0, None, OP.add)
    m_tb = ts([m_ti], T.tb[:, 128:256], T.ti[:, 128:256], -256.0, None, OP.add)
    c_k1 = ts([x], CO[:, 1:2], CO[:, 2:3], -100.0, None, OP.add)
    ts([mo, c_k0], so[:, 0:128], po[:, 0:128], CO[:, 0:1], None, OP.is_equal)
    m_s1 = ts([c_k1], so[:, 128:256], po[:, 0:128], CO[:, 1:2], None, OP.is_equal)
    if r > 0:
        k = ts([k, gt], CO[:, 8:9], CO[:, 5:6], 32.0, CO[:, 7:8], OP.mult, OP.add)
    if r > 1:
        ts([m_x], T.selc[:, 0:128], T.px[:, 0:128], CO[:, 0:1], CODE, OP.is_equal, OP.mult)
        m_sf = ts([], T.selc[:, 128:256], T.px[:, 0:128], CO[:, 1:2], CODE, OP.is_equal, OP.mult)
    c_mask = ts([c_row], T.mask[:], T.rowf[:, 0:16], CF[:, 1:2], None, OP.is_equal)
    if r > 0:
        c_k9 = ts([k], CO[:, 9:10], CO[:, 8:9], 8.0, None, OP.add)
    c_tri = do("p", [c_bo], lambda: g.affine_select(T.tri[:], T.bo[:], [[1, 128]], OP.is_gt, 0.0, 0, -1))

    def late_constants():
        th = ts([], T.thr[:], T.rowf[:, 0:4], -3.0, CODE, OP.add, OP.mult)
        return ts([], T.gind[:], T.rowf[:, 0:8], CF[:, 0:1], None, OP.is_equal), th

    def window_ab(sel, tb, w, deps):
        a = do("t", deps, lambda: mm(T.pwa[:, 0:256], sel[:, 0:128], tb[:], True, True))
        b = do("t", [], lambda: mm(T.pwb[:, 0:256], sel[:, 128:256], tb[:], True, True))
        sa = do("s", [a], lambda: act(w[:, 0:256], T.pwa[:, 0:256], AF.Copy))
        vb = do("v", [b], lambda: vec.tensor_copy(w[:, 256:512], T.pwb[:, 0:256]))
        return [sa, vb]

    def window_all(sel, tb, deps, pairs):
        for h in range(2):
            c = slice(256 * h, 256 * h + 256)
            d = do("t", deps, lambda: mm(T.pwa[:, c], sel[:, 128 * h:128 * h + 128], tb[:], True, not pairs))
            if pairs:
                d = do("t", [c_ramp, c_evl], lambda: mm(T.pwa[:, c], T.evl[:], T.ramp[:, c], False, True))
        return d

    def window_out(w, d):
        return [do("s", [d], lambda: act(w[:], T.pwa[:], AF.Copy))]

    def em_float():
        return ts([l_em], T.emf[:], T.emi[:], -4 * CODE, None, OP.add)

    def code_parts(c0, c1):
        c = slice(c0, c1)

        def a0():
            ts([l_em], T.hi[:, c], T.emi[:, c], 18, None, OP.arith_shift_right)

        def a1():
            ts([l_nx], T.pb[:, c], T.nxi[:, c], 2048.0, 64.0, OP.is_lt, OP.mult)

        def a2():
            ts([], T.ci[:, c], T.nxi[:, c], 9, None, OP.arith_shift_right)
        return [a0, a1, a2]

    def code_rest():
        n = do("v", [("v", cnt["v"])], lambda: vec.tensor_tensor(T.pb[:, 256:512], T.hi[:], T.pb[:, 0:256], OP.min))
        return do("v", [n], lambda: vec.tensor_tensor(T.za[:], T.ci[:], T.pb[:, 256:512], OP.subtract))

    def code_mm(banks, sf, em, sc, za, dep_em, dep_za):
        def numbers(h):
            c = slice(128 * h, 128 * h + 128)
            return lambda: do("t", dep_em, lambda: mm(banks[h][:, 0:256], sf[:, c], em[:], True, False))

        def counts():
            for h in range(2):
                c = slice(128 * h, 128 * h + 128)
                d = do("t", dep_za, lambda: mm(banks[h][:, 0:256], sc[:, c], za[:], False, True))
            return d
        return [numbers(0), numbers(1), counts]

    def code_out(banks, w, d):
        do("s", [d], lambda: act(w[:, 0:256], banks[0][:, 0:256], AF.Copy))
        return do("s", [d], lambda: act(w[:, 256:512], banks[1][:, 0:256], AF.Copy))

    def scaled(out, src, by, deps):
        return do("s", deps, lambda: act(out[:], src[:], AF.Copy, scale=by))

    em_box, id_box = [None], [None, None]
    each = 1 if r == 1 else 2

    def lists():
        sf = do("v", [l_sc], lambda: vec.tensor_copy(CO[:, 3:4], T.syc[:]))
        ti = ts([l_tp], T.tpi[:], T.tp[:], 511, None, OP.bitwise_and)
        if r > 1:
            em_box[0] = em_float()
        d = ts([sf, c_mask], T.d16[:], T.mask[:], CO[:, 3:4], None, OP.mult)
        am = do("t", [d], lambda: mm(T.py[:, 64:80], T.bo[:], T.d16[:], True, True))
        tq = do("v", [ti], lambda: vec.tensor_copy(T.tq[:, 16:272], T.tpi[:]))
        id_box[0] = ts([c_pf], T.idn[:], T.rowf[:], T.pf[:], None, OP.is_equal)
        id_box[1] = ts([], T.pm[:], T.rowf[:, 0:8], CF[:, 2:3], None, OP.is_equal)
        n = 32 // each
        ts([am, c_k9], T.ot[:, 0:n:2], T.py[:, 64:80:each], 32.0, CO[:, 8:9], OP.mult, OP.add)
        do("v", [tq], lambda: vec.transpose(T.tab[:, 0:256], T.tq[:, 16:272]))
        o = ts([], T.ot[:, 1:n:2], T.py[:, 64:80:each], 32.0, CO[:, 9:10], OP.mult, OP.add)
        tr = do("v", [tq], lambda: vec.transpose(T.tab[:, 256:544], T.tq[:, 0:288]))
        n0, n1 = (2 * FOURS[0], 30) if r == 1 else (2 * first, 16)
        return do("v", [tr, o], lambda: vec.tensor_copy(T.lt[:, 16 * n0:16 * n1], T.tab[:].indirect(T.ot[:, n0:n1])))

    def joined(n):
        return T.cp[:, 512 * n:512 * n + 512]

    def join(n, win, j, deps, qn, m):
        i = 32 * (j // each)
        out, src = joined(n), win.indirect(T.lt[:, i:i + 32])
        keep = 1.0 if m is None else T.pm[:, m:m + 1]
        if qn == "v":
            return ts(deps + id_box, out, src, keep, None, OP.mult)
        return do("s", deps + id_box, lambda: act(out, src, AF.Copy, scale=keep))

    def gather(win, at, deps, k, col):
        b = col - k
        tile, x0, d = at
        return (T.tt, col, ts([d] + deps, T.tt[:, b:b + 16], win.indirect(tile[:, x0:x0 + 1]), 256.0, None, OP.add))

    def code_at(qn, reads, j, ewin, edep, ee):
        tile, x0, d = reads[j]
        b = 0 if j == 0 else 16 * j + 16
        out, src = ee[:, b:b + 16], ewin[:].indirect(tile[:, x0:x0 + 1])
        if qn == "v":
            return ts([d, edep, c_mask], out, src, T.mask[:, j:j + 1], None, OP.mult)
        return do("s", [d, edep, c_mask], lambda: act(out, src, AF.Copy, scale=T.mask[:, j:j + 1]))

    def follow(reads, ewin, edep, ee, steps):
        for j in steps:
            last = code_at("s", reads, j, ewin, edep, ee)
        return last

    def string(q, at, w, wdep, pw, pdep, reg, hooks, last_too):
        reads = []
        for j in range(16):
            reads.append(at)
            pair = j >= 2 * FIRST.get(q, 8)
            if not (pair and j % 2):
                k, col = (j - 1) % 16, reg + 16 + 18 * j
                if pair:
                    at = gather(pw(j // 2), at, pdep(j // 2), k, col)
                elif j < 15 or last_too:
                    at = gather(w[:], at, wdep, k, col)
            play(hooks.get(j, []))
        return reads, at

    gd, ed_, ydep = {}, {}, [None, 0]

    def total(ee, last, out):
        return do("v", last, lambda: vec.tensor_reduce(out[:], ee[:, 15:271:17], AxisListType.X, OP.add))

    def gates(q, code, dep):
        gd[q] = ts([dep, c_thr], T["g4%d" % q][:], T.thr[:], code[:], None, OP.is_le)

    def digits(q, code, dep):
        qi, di, ep = T["qi%d" % q], T["di%d" % q], T["ep%d" % q]
        box = {}

        def d0():
            box[0] = do("v", [dep], lambda: vec.tensor_copy(qi[:], code[:]))

        def d1():
            ts([box[0]], di[:, 0:1], qi[:], 63, None, OP.bitwise_and)
            ts([], di[:, 1:2], qi[:], 6, 63, OP.arith_shift_right, OP.bitwise_and)

        def d2():
            ts([], di[:, 2:3], qi[:], 12, 63, OP.arith_shift_right, OP.bitwise_and)
            box[1] = ts([], di[:, 3:4], qi[:], 18, 63, OP.arith_shift_right, OP.bitwise_and)

        def d3():
            ed_[q] = do("v", [box[1], gd[q]], lambda: vec.tensor_tensor(ep[:], di[:], T["g4%d" % q][:], OP.mult))
        return [d0, d1, d2, d3]

    def decode(q, code, dep):
        return [lambda: gates(q, code, dep)] + digits(q, code, dep)

    banks = {0: T.pb, 1: T.pc, 2: T.pcm, 3: T.pb}
    free = {}
    begun = {}
    bdep = {}

    def count(q, b, stop=False):
        n = 1 if q == 3 else 4
        for m in range(0, 4, n):
            bdep[q] = do("t", [gd[b], c_tri, free.get(q)], lambda: mm(
                banks[q][:, 0:n], (T.tri if b == q else T.bo)[:], T["g4%d" % b][:, m:m + n], q not in begun, stop and m + n == 4))
            begun[q] = True

    def position(q):
        if q < 3:
            bdep[q] = do("v", [bdep[q]], lambda: vec.tensor_reduce(T.pos[:, q:q + 1], banks[q][:, 0:4], AxisListType.X, OP.add))

    def place(q, final):
        oh, ep = T["oh%d" % q], T["ep%d" % q]

        def one(m):
            o = ts([bdep[q], ed_[q], c_io], oh[:, 32 * m:32 * m + 32], T.io4[:, 32 * m:32 * m + 32],
                   T.pos[:, q:q + 1] if q < 3 else banks[q][:, 0:1], ep[:, m:m + 1], OP.is_equal, OP.mult)
            ydep[0] = do("t", [o, c_gi], lambda: mm(
                T.py[0:8, 0:32], T.gind[:], oh[:, 32 * m:32 * m + 32], ydep[1] == 0, final and m == 3))
            ydep[1] += 1
        return [lambda: position(q), lambda: one(0), lambda: one(1), lambda: one(2), lambda: one(3)]

    if r == 0:
        wdep = window_ab(T.sel, T.tb, T.w, [m_s1, m_tb])
        sfd = scaled(T.self, T.sel, 1.0, [m_s1])
        scd = scaled(T.selc, T.sel, CODE, [m_s1])
        parts = []
        for c in range(0, 256, 64):
            parts += code_parts(c, c + 64)
        hooks = {}
        for n in range(len(parts)):
            hooks[n + 2] = [parts[n]]
        reads, at = string(0, (T.zero, 0, c_zero), T.w, wdep, None, None, 0, hooks, True)
        s1 = T.tt[:, at[1]:at[1] + 2]
        send([at[2]], [2, 3], "s1", s1, "as1")
        send([], [1], "s1", s1, "as1")
        emd = em_float()
        zad = code_rest()
        cb = (T.pew, T.pcm)
        fs = code_mm(cb, T.self, T.emf, T.selc, T.za, [sfd, emd], [scd, zad])
        play(fs[:2])
        ed = code_out(cb, T.e, fs[2]())
        c_gi, c_thr = late_constants()
        last = follow(reads, T.e, ed, T.eea, range(0, 16, 2))
        for j in range(1, 16, 2):
            last_v = code_at("v", reads, j, T.e, ed, T.eea)
        oc = total(T.eea, [last, last_v], T.oca)
        send([oc], [2, 3, 1], "rc0", T.oca[:], "arc0")
        play(decode(0, T.oca, oc))
        count(0, 0, True)
        play(place(0, False))
        count(1, 0)
        a1 = arrive(1, "arc1")
        gates(1, T.rc1, a1)
        count(1, 1, True)
        play(digits(1, T.rc1, a1))
        play(place(1, True))
    elif r == 1:
        wdep = window_out(T.w, window_all(T.sel, T.tb, [m_s1, m_tb], False))
        send(wdep, [2, 3], "w1", T.w[:], "aw1", True)
        ltd = lists()
        va, sa = FOURS
        dv = join(0, T.w[:], va + 2, wdep + [ltd], "v", None)
        ds = join(3, T.w[:], sa + 2, wdep + [ltd], "s", None)
        emd = em_float()
        dv = join(1, joined(0), va + 1, [dv], "v", None)
        ds = join(4, joined(3), sa + 1, [ds], "s", None)
        parts = code_parts(0, 256)
        parts[0]()
        dv = join(2, joined(1), va, [dv], "v", (va + 3) // 2)
        ds = join(5, joined(4), sa, [ds], "s", (sa + 3) // 2)
        play(parts[1:])
        md = []
        for n, d in ((2, dv), (5, ds)):
            for h in range(2):
                x = 512 * n + 256 * h
                md.append(do("t", [d] + id_box, lambda: mm((T.pcm, T.px)[h][:, 0:256], T.idn[:], T.cp[:, x:x + 256],
                                                           n == 2, n == 5)))
        cmd = [do("v", [md[2]], lambda: vec.tensor_copy(T.cpm[:, 0:256], T.pcm[:, 0:256])),
               do("s", [md[3]], lambda: act(T.cpm[:, 256:512], T.px[:, 0:256], AF.Copy))]
        free[2] = cmd[0]
        send(cmd, [2, 3], "cp1", T.cpm[:], "acp1", True)
        sfd = scaled(T.self, T.sel, 1.0, [m_s1])
        scd = scaled(T.selc, T.sel, CODE, [m_s1])
        zad = code_rest()
        cb = (T.pew, T.pwb)
        fs = code_mm(cb, T.self, T.emf, T.selc, T.za, [sfd, emd], [scd, zad])
        play(fs[:2])
        ed = code_out(cb, T.e, fs[2]())
        reads = string(1, (T.s1, 0, arrive(0, "as1")), T.w, wdep, None, None, 0, {}, False)[0]
        last = follow(reads, T.e, ed, T.eea, range(15))
        c_gi, c_thr = late_constants()
        last_v = code_at("v", reads, 15, T.e, ed, T.eea)
        oc = total(T.eea, [last, last_v], T.oca)
        send([oc], [2, 3, 0], "rc1", T.oca[:], "arc1", True)
        play(decode(1, T.oca, oc))
        count(1, 1)
        a0 = arrive(0, "arc0")
        gates(0, T.rc0, a0)
        count(1, 0, True)
        count(0, 0, True)
        count(2, 0)
        count(2, 1)
        play(digits(0, T.rc0, a0))
        play(place(0, False))
        play(place(1, False))
        a2 = arrive(3, "arc2")
        gates(2, T.rc2, a2)
        count(2, 2, True)
        play(digits(2, T.rc2, a2))
        play(place(2, True))
    else:
        o = 5 - r
        wdep = window_out(T.w, window_all(T.selo, T.tb, [m_s1, m_tb], True))
        sfd = scaled(T.self, T.selc, 1.0 / CODE, [m_sf])
        send([m_sf], [o], "selx", T.selc[:], "aselx")
        ltd = lists()
        emd = em_box[0]
        send([emd], [o], "emx", T.emf[:], "aemx")
        if first:
            send(wdep, [o], "wx", T.w[:], "awx")
        on_s, made = list(range(first, 5)), {}
        axs = arrive(o, "aselx")
        between = 2 if r == 3 else len(on_s)
        for m in on_s[:between]:
            made[m] = join(m, T.w[:], 2 * m, wdep + [ltd], "s", m)
        sfx = scaled(T.selfx, T.selx, 1.0 / CODE, [axs])
        for m in on_s[between:]:
            made[m] = join(m, T.w[:], 2 * m, wdep + [ltd], "s", m)
        for m in (5, 6, 7):
            made[m] = join(m, T.w[:], 2 * m, wdep + [ltd], "v", m)
        play(code_parts(0, 256))
        zad = code_rest()
        send([zad], [o], "zax", T.za[:], "azax")
        own_banks, other_banks = (T.pew, T.pwb), (T.px, T.pwa)
        axe, axz = arrive(o, "aemx"), arrive(o, "azax")
        own = code_mm(own_banks, T.self, T.emf, T.selc, T.za, [sfd, emd], [zad])
        other = code_mm(other_banks, T.selfx, T.emx, T.selx, T.zax, [sfx, axe, m_sf, wdep[0]], [axz])
        codes = {r: (own, own_banks, T.e), o: (other, other_banks, T.ex)}
        code2, code3 = codes[2][0], codes[3][0]
        e2, e3 = codes[2][2], codes[3][2]
        order = [5, on_s[0], 6, on_s[1], 7] + on_s[2:]
        for n in range(len(order)):
            if r == 3 and n == 5:
                code2.pop(0)()
            m = order[n]
            md = do("t", [made[m]] + id_box, lambda: mm(T.pcm[:], T.idn[:], joined(m), n == 0, n == len(order) - 1))
        cmd = do("s", [md], lambda: act(T.cpm[:], T.pcm[:], AF.Copy))
        free[2] = cmd
        send([cmd], [o], "cpx", T.cpm[:], "acpx")
        play(code2[:-1])
        e2d = code_out(codes[2][1], e2, code2[-1]())
        play(code3[:-1])
        m3 = code3[-1]()
        aw1, acp1 = [arrive(1, "aw1", True)], [arrive(1, "acp1", True)]
        awx, acpx = [arrive(o, "awx")] if FIRST[o] else [], [arrive(o, "acpx")]
        at = (T.s1, 0, arrive(0, "as1"))
        for j in range(FOURS[0]):
            at = gather(T.w1[:], at, aw1, (j - 1) % 16, 16 + 18 * j)
            if j == 0:
                c_gi, c_thr = late_constants()
        for j in FOURS:
            at = gather(T.cp1[:], at, acp1, j - 1, 16 + 18 * j)
        runs = {r: (T.w, wdep, joined, lambda m: [made[m]]), o: (T.wx, awx, lambda m: T.cpx[:], lambda m: acpx)}
        reads, at = string(2, at, *runs[2], 320, {}, True)
        last = follow(reads, e2, e2d, T.eea, range(16))
        e3d = code_out(codes[3][1], e3, m3)
        a0, a1 = arrive(0, "arc0"), arrive(1, "arc1", True)
        box = {}

        def g0():
            gates(0, T.rc0, a0)
            for q in range(1 if r == 2 else 2, 4):
                count(q, 0)

        def t2():
            box[2] = total(T.eea, [last], T.oca)
            if r == 3:
                send([box[2]], [1], "rc2", T.oca[:], "arc2")

        def g2():
            gates(2, T.oca, box[2])
            count(2, 2)
            count(3, 2)

        def g1():
            gates(1, T.rc1, a1)
            if r == 2:
                count(1, 1, True)
            count(2, 1, True)
            count(3, 1)
        D2, p2 = digits(2, T.oca, None), place(2, False)
        D1, p1 = (digits(1, T.rc1, a1), place(1, False)) if r == 2 else ([], [])
        hooks = {0: [g0], 2: [t2], 4: [g2] + D2[:1], 6: D2[1:2], 8: D2[2:3], 10: D2[3:], 12: [g1] + D1[:1], 14: D1[1:3]}
        reads3 = string(3, at, *runs[3], 640, hooks, False)[0]
        last3 = follow(reads3, e3, e3d, T.eeb, range(15))
        last_v = code_at("v", reads3, 15, e3, e3d, T.eeb)
        play(D1[3:])
        oc = total(T.eeb, [last3, last_v], T.ocb)
        play(p2[:1] + p1[:1])
        D3 = digits(3, T.ocb, oc)
        D3[0]()
        gates(3, T.ocb, oc)
        count(3, 3, True)
        play(p2[1:4])
        play(D3[1:3])
        play(p2[4:] + p1[1:3])
        D3[3]()
        play(p1[3:])
        if r == 3:
            for b in (0, 2, 1, 3):
                zd = do("t", [gd[b], e3d], lambda: mm(T.pew[0:8, 0:4], T.gind[:], T["g4%d" % b][:], b == 0, b == 3))
        play(place(3, True))
        if r == 3:
            zr = do("v", [zd], lambda: vec.tensor_reduce(T.zed[:], T.pew[0:8, 0:4], AxisListType.X, OP.add))
            nd = ts([zr, c_io], T.neg[:], T.io4[0:8, 0:32], T.zed[:], -1.0, OP.is_ge, OP.mult)
    if r == 3:
        yd = do("v", [ydep[0], nd], lambda: vec.tensor_tensor(T.ysb[:], T.py[0:8, 0:32], T.neg[:], OP.add))
    else:
        yd = do("v", [ydep[0]], lambda: vec.tensor_copy(T.ysb[:], T.py[0:8, 0:32]))
    dma("y", [yd], "st", T.y[:], T.ysb[:])
    for sn in list(cnt):
        if sn != "st":
            waits("p", [(sn, cnt[sn])])
    waits("p", [("st", 16)])
